import numpy as np
import ml_dtypes


def mxq(x, axis, fmt="e4m3"):
    dtype, down = {"e4m3": (ml_dtypes.float8_e4m3fn, 7), "e5m2": (ml_dtypes.float8_e5m2, 14)}[fmt]
    v = np.moveaxis(np.asarray(x, np.float32).astype(ml_dtypes.bfloat16).astype(np.float64), axis, -1)
    blocks = v.reshape(v.shape[:-1] + (-1, 32))
    amax = np.abs(blocks).max(-1, keepdims=True)
    byte = np.maximum(np.where(amax > 0, np.frexp(amax)[1] - 1 + 127, 0) - down, 1)
    scale = np.exp2(byte - 127.0)
    codes = (blocks / scale).astype(np.float32).astype(dtype).astype(np.float64)
    return np.moveaxis((codes * scale).reshape(v.shape), -1, axis)


WIDE = False


def mx_kscale(k):
    if not WIDE:
        return np.ones(k)
    levels = np.array([10, -10, 5, -5, 0])
    if k % 512:
        return np.exp2(np.random.permutation(np.resize(levels, k // 32))).repeat(32)
    a = np.empty((k // 512, 16))
    for p in range(k // 512):
        a[p, :8] = np.random.permutation(np.resize(levels, 8))
        for g in range(8):
            far = levels[np.abs(levels - a[p, g]) >= 10]
            a[p, g + 8] = far[np.random.randint(len(far))]
    return np.exp2(a.ravel()).repeat(32)


BF16 = ml_dtypes.bfloat16


def bf(x):
    return np.asarray(x, np.float32).astype(BF16)


def f64(x):
    return np.asarray(x).astype(np.float64)


E2M1 = np.array([0.0, 0.5, 1.0, 1.5, 2.0, 3.0, 4.0, 6.0, -0.0, -0.5, -1.0, -1.5, -2.0, -3.0, -4.0, -6.0])


def pack_weight(w, fmt):
    k, n = w.shape
    w = f64(bf(w)).reshape(k // 32, 32, n)
    amax = np.abs(w).max(1)
    if fmt == "e4m3":
        byte = np.frexp(amax)[1] - 1 + 127 - 7
    else:
        mant, ex = np.frexp(amax / 6.0)
        byte = np.where(mant > 0.5, ex, ex - 1) + 127
    byte = np.clip(np.where(amax > 0, byte, 1), 1, 254)
    scaled = (w * np.exp2(127.0 - byte)[:, None, :]).reshape(k, n).astype(np.float32)
    by_word = np.ascontiguousarray(scaled.reshape(k // 512, 128, 4, n).transpose(0, 1, 3, 2))
    if fmt == "e4m3":
        words = by_word.astype(ml_dtypes.float8_e4m3fn).view(np.uint8)
    else:
        c = by_word.astype(ml_dtypes.float4_e2m1fn).view(np.uint8) & 0xF
        words = c[..., 0::2] | (c[..., 1::2] << 4)
    return np.ascontiguousarray(words), np.ascontiguousarray(byte.astype(np.uint8).reshape(k // 512, 16, n))


def unpack_weight(words, scales, fmt):
    g, p, n, _ = words.shape
    if fmt == "e4m3":
        vals = np.ascontiguousarray(words).view(ml_dtypes.float8_e4m3fn).astype(np.float64)
    else:
        nib = np.empty((g, p, n, 4), np.uint8)
        nib[..., 0::2] = words & 0xF
        nib[..., 1::2] = words >> 4
        vals = E2M1[nib]
    vals = vals * np.repeat(np.exp2(scales.astype(np.float64) - 127.0), 8, axis=1)[..., None]
    return vals.transpose(0, 1, 3, 2).reshape(g * 512, n)
def pack4(w):
    words, scales = pack_weight(w, "e2m1")
    return words.reshape(words.shape[0], 128, -1), scales


def unpack4(words, scales):
    return unpack_weight(words.reshape(words.shape[0], 128, -1, 2), scales, "e2m1")


E4M3FN = np.array([(-1.0 if i & 128 else 1.0) * ((1.0 + (i & 7) / 8.0) * 2.0 ** (((i >> 3) & 15) - 7) if i & 120 else (i & 7) * 2.0 ** -9) for i in range(256)])


def e4m3fn_bytes(y):
    return np.clip(np.asarray(y, np.float64), -448.0, 448.0).astype(np.float32).astype(ml_dtypes.float8_e4m3fn).view(np.uint8)


def e4m3fn_values(b):
    return E4M3FN[b]


T, K, N, M, C, L = 4096, 1024, 1024, 1024, 8, 128

KEEP = 0.875


def setup_inputs():
    s, t = mx_kscale(K), mx_kscale(N)
    x = np.random.standard_normal((T, K)) * s
    x_scale = (np.abs(x).reshape(T, K // L, L).max(axis=2) / 448).astype(np.float32)
    x_bytes = e4m3fn_bytes(x / np.repeat(f64(x_scale), L, axis=1))
    w = np.random.standard_normal((K, N)) / np.sqrt(K) / s[:, None] * t
    query = 1.5 * np.random.standard_normal((N, M)) / np.sqrt(N) / t[:, None]
    query_words, query_scales = pack4(query)
    return {"x_bytes": x_bytes,
            "x_scale": x_scale,
            "w": bf(w),
            "query_words": query_words,
            "query_scales": query_scales,
            "mask": bf(np.random.random((M, T // C)) < KEEP)}


def reference(x_bytes, x_scale, w, query_words, query_scales, mask):
    x = e4m3fn_values(x_bytes) * np.repeat(f64(x_scale), L, axis=1)
    h = mxq(x, 1, "e4m3") @ mxq(f64(w), 0, "e4m3")
    f = np.maximum(h, 0.0)
    a = f.reshape(T // C, C, N).mean(axis=1)
    query = unpack4(query_words, query_scales)
    z = query.T @ mxq(a, 1, "e4m3").T
    return np.exp(z) * f64(mask)

@@ -1,0 +1,274 @@
+from contextlib import ExitStack
+
+import concourse.mybir as mybir
+from concourse.masks import make_identity
+
+F32 = mybir.dt.float32
+BF16 = mybir.dt.bfloat16
+U32 = mybir.dt.uint32
+I32 = mybir.dt.int32
+U8 = mybir.dt.uint8
+FP8 = mybir.dt.float8_e4m3fn
+FP8X4 = mybir.dt.float8_e4m3fn_x4
+FP4X4 = mybir.dt.float4_e2m1fn_x4
+ALU = mybir.AluOpType
+ACT = mybir.ActivationFunctionType
+
+T, K, N, M, C = 4096, 1024, 1024, 1024, 8
+P = 128
+FLOPS = 2 * T * K * N + 2 * M * N * (T // C)
+
+
+def build_order():
+    o=[]
+    o+=[('L','xs0',64),('L','x0',256),('L','w00',512),('L','w10',512),('L','x1',256),('L','x2',256),('L','w01',512),('L','w11',512),('L','x3',256),('L','x4',256),('L','xs1',64)]
+    o+=[('L','x%d'%s,256) for s in range(5,8)]+[('L','q',600),('L','mask',1024)]+[('L','x%d'%s,256) for s in range(8,16)]
+    V,S='V','S'
+    o+=[('WV',0,0,V),('WV',0,1,V),('WS',0,0,S),('WS',0,1,V),('T',0,0),('T',0,1)]
+    o+=[('WI',0,0,0,V),('C',0,0,S),('C',0,1,S),('WI',0,0,1,V),('WI',1,0,0,V),('WQ',0,0,0),('WQ',0,0,1),('WQ',1,0,0),('Q',0),('WS',1,0,S),('WS',1,1,S),('WI',1,0,1,V),('WV',1,0,V),('WV',1,1,V),('WQ',1,0,1),('WV',2,0,V),('WV',2,1,V)]
+    o+=[('M',0,0),('T',1,0),('T',1,1),('M',0,1),('WS',2,0,S),('C',1,0,S),('C',1,1,S),('WI',0,1,0,V),('WS',2,1,S),('WI',1,1,0,V),('WQ',0,1,0),('Q',1),('WQ',1,1,0),('R',0,0,S),('R',0,1,S),('T',2,0),('T',2,1),('M',1,0),('M',1,1),('WI',0,1,1,V),('C',2,0,S),('C',2,1,S),('WI',1,1,1,V),('WQ',0,1,1),('WV',3,0,V),('WQ',1,1,1),('M',0,2),('M',0,3),('WS',3,0,S),('WS',3,1,S),('WV',3,1,V),('R',1,0,V),('Q',2),('R',0,2,S),('R',0,3,S),('R',1,1,V),('M',1,2),('M',1,3),('WS',4,0,S),('WS',4,1,S),('WV',4,0,V),('WV',4,1,V)]
+    pend=[('R',1,2,V),('R',1,3,V)]
+    for i in range(2,14):
+        first = i==8
+        n=i+3
+        o+=[('T',i+1,0),('T',i+1,1)]
+        o+=pend; pend=[]
+        o+=[('C',i+1,0,S),('C',i+1,1,S)]
+        if first:
+            o+=[('WV',n,0,V),('WV',n,1,V),('WS',n,0,V),('Q',i+1),('WS',n,1,V),('AI',0,0,0,V),('AI',0,0,1,V),('AI',0,1,0,V),('AQ',0,0),('AI',0,1,1,V),('WV',n+1,0,V),('AQ',0,1)]
+            o+=[('M',i,0),('R',i,0,S),('M',i,1),('R',i,1,S),('M',i,2),('R',i,2,S),('M',i,3),('R',i,3,S)]
+            continue
+        if n<16:
+            if i!=9: o+=[('WV',n,0,V)]
+            o+=[('WS',n,0,S),('WS',n,1,S),('WV',n,1,S if SW(i) else V)]
+        o+=[('M',i,0),('R',i,0,V),('M',i,1),('R',i,1,V),('Q',i+1),('M',i,2),('R',i,2,V),('M',i,3)]
+        pend=[('R',i,3,V)]
+        if 9<=i<=12:
+            o+=[('Z',0,i-9),('E',0,i-9)]; pend+=[('K',0,i-9,V),('ST',0,i-9)]
+    o+=[('T',15,0),('T',15,1)]+pend+[('C',15,0,S),('C',15,1,S),('M',14,0),('M',14,1),('R',14,0,V),('Q',15),('R',14,1,V),('M',14,2),('M',15,0),('M',15,1),('M',14,3),('M',15,2),('M',15,3)]
+    o+=[('R',14,2,V),('R',15,0,V),('R',15,1,V),('R',14,3,V),('AI',1,0,0,S),('AI',1,0,1,S),('R',15,2,V),('R',15,3,V),('AQ',1,0),('AI',1,1,0,V),('AI',1,1,1,S),('AQ',1,1)]
+    for q in range(4): o+=[('Z',1,q),('E',1,q),('K',1,q,V),('ST',1,q)]
+    return o
+def SW(i): return i<8 or i>9
+
+
+def tile_masked_block_scores_d4_kernel(tc, x_bytes, x_scale, w, query_words, query_scales, mask, out):
+    nc = tc.nc
+    with ExitStack() as ctx:
+        keep = ctx.enter_context(tc.tile_pool(name="keep", bufs=1))
+        work = ctx.enter_context(tc.tile_pool(name="work", bufs=3))
+        tps = ctx.enter_context(tc.psum_pool(name="tps", bufs=1))
+        mps = ctx.enter_context(tc.psum_pool(name="mps", bufs=6))
+
+        ident = keep.tile([P, P], F32, name="ident")
+        make_identity(nc, ident[:])
+        q_scales = keep.tile([P, 2, M], U8, name="q_scales", align_bytes=64)
+        nc.gpsimd.memset(q_scales[:].rearrange("p g n -> p (g n)").bitcast(I32), 0)
+        q_words = keep.tile([P, 2, 2 * M], U8, name="q_words", align_bytes=64)
+        mask_sb = keep.tile([P, 8, 512], BF16, name="mask_sb")
+        xs = [keep.tile([P, 2, 64], F32, name="xs%d" % h) for h in range(2)]
+        xb = [keep.tile([P, 2, K], U8, name="xbytes%d" % s) for s in range(16)]
+        w_raw = {(g, G): keep.tile([P, 4, 512], BF16, name="w_raw%d%d" % (g, G)) for g in range(2) for G in range(2)}
+        w_codes = {}
+        w_scales = {}
+        for g in range(2):
+            for G in range(2):
+                for tp in range(2):
+                    w_codes[g, G, tp] = keep.tile([P, 256], U32, name="w_codes%d%d%d" % (g, G, tp), align_bytes=64)
+                    w_scales[g, G, tp] = keep.tile([P, 256], U8, name="w_scales%d%d%d" % (g, G, tp), align_bytes=64)
+        acc2 = {(h, G): keep.tile([P, 4, 256], F32, name="acc%d%d" % (h, G)) for h in range(2) for G in range(2)}
+        warm = keep.tile([P, 2], F32, name="warm")
+
+        x_view = x_bytes.rearrange("(h c p j) k -> h j p c k", h=2, c=2, p=P)
+        xs_view = x_scale.rearrange("(h c p j) b -> h p c (j b)", h=2, c=2, p=P)
+        out_view = out.rearrange("(t p) b -> p t b", p=P)
+        live = {}
+
+        ctx.enter_context(tc.manual_schedule())
+        nc.vector.memset(warm[:, 0:1], 0.0)
+        nc.scalar.activation(out=warm[:, 1:2], in_=warm[:, 0:1], func=ACT.Exp)
+
+        def load(name):
+            if name.startswith("xs"):
+                h = int(name[2:])
+                nc.sync.dma_start(out=xs[h][:], in_=xs_view[h])
+            elif name.startswith("x"):
+                s = int(name[1:])
+                nc.sync.dma_start(out=xb[s][:], in_=x_view[s // 8, s % 8])
+            elif name.startswith("w"):
+                g, G = int(name[1]), int(name[2])
+                rows = w[512 * g : 512 * (g + 1), 512 * G : 512 * (G + 1)]
+                if g == 0:
+                    by_half = rows.rearrange("(b u r) n -> u b r n", u=2, r=16)
+                    for u in range(2):
+                        nc.sync.dma_start(out=w_raw[g, G][:, 2 * u : 2 * u + 2, :], in_=by_half[u])
+                else:
+                    nc.sync.dma_start(out=w_raw[g, G][:], in_=rows.rearrange("(p j) n -> p j n", j=4))
+            elif name == "q":
+                for quad in range(4):
+                    nc.sync.dma_start(
+                        out=q_scales[32 * quad : 32 * quad + 4, :, :].bitcast(I32),
+                        in_=query_scales[:, 4 * quad : 4 * quad + 4, :].rearrange("g r n -> r g n").bitcast(I32),
+                    )
+                nc.sync.dma_start(out=q_words[:].bitcast(I32), in_=query_words.rearrange("g p n -> p g n").bitcast(I32))
+            else:
+                nc.sync.dma_start(out=mask_sb[:], in_=mask.rearrange("(t p) b -> p t b", p=P))
+
+        def wide_tile(s, g, c):
+            live["wide", s, g, c] = work.tile([P, 512], BF16, name="wide%d%d" % (g, c), bufs=4)
+            return live["wide", s, g, c]
+
+        def widen_plain(dst, s, g, c, eng):
+            for q in range(4):
+                blk = 4 * g + q
+                src = xb[s][:, c, P * blk : P * (blk + 1)].bitcast(FP8)
+                scale = xs[s // 8][:, c, 8 * (s % 8) + blk : 8 * (s % 8) + blk + 1]
+                if eng == "S":
+                    nc.scalar.activation(out=dst[:, P * q : P * (q + 1)], in_=src, func=ACT.Copy, scale=scale)
+                else:
+                    nc.vector.tensor_scalar(out=dst[:, P * q : P * (q + 1)], in0=src, scalar1=scale, scalar2=None, op0=ALU.mult)
+
+        def widen_split(s, c, eng):
+            dst = wide_tile(s, 0, c)
+            if eng == "S":
+                plain = work.tile([P, 512], BF16, name="plain", bufs=2)
+                widen_plain(plain, s, 0, c, "S")
+                nc.scalar.copy(
+                    out=dst[:].rearrange("p (u b e) -> p u b e", u=2, e=16),
+                    in_=plain[:].rearrange("p (b u e) -> p u b e", u=2, e=16),
+                )
+                return
+            halves = dst[:].rearrange("p (u b e) -> p b u e", u=2, e=16)
+            for q in range(4):
+                src = xb[s][:, c, P * q : P * (q + 1)].bitcast(FP8).rearrange("p (b u e) -> p b u e", u=2, e=16)
+                scale = xs[s // 8][:, c, 8 * (s % 8) + q : 8 * (s % 8) + q + 1]
+                nc.vector.tensor_scalar(out=halves[:, 4 * q : 4 * q + 4], in0=src, scalar1=scale, scalar2=None, op0=ALU.mult)
+
+        def turn(s, g):
+            bank = tps.tile([P, 2, 2, P], F32, name="turned%d" % g)
+            live["turned", s, g] = bank
+            for c in range(2):
+                words = live["wide", s, g, c][:].bitcast(F32)
+                for u in range(2):
+                    src = words[:, P * u : P * (u + 1)] if g == 0 else words[:, u : 2 * P : 2]
+                    nc.tensor.transpose(bank[:, c, u, :], src, ident[:])
+
+        def copy_out(s, g, eng):
+            if g == 0:
+                live["grouped", s] = work.tile([P, 2, 1024], BF16, name="x_grouped", align_bytes=64)
+            dst = live["grouped", s][:, g, :].bitcast(F32).rearrange("p (c r u) -> p c r u", c=2, u=2)
+            src = live["turned", s, g][:].rearrange("p c u r -> p c r u")
+            if eng == "S":
+                nc.scalar.copy(out=dst, in_=src)
+            else:
+                nc.vector.tensor_copy(out=dst, in_=src)
+
+        def quant_x(s):
+            codes = work.tile([P, 512], U32, name="x_codes", align_bytes=64, bufs=4)
+            scales = work.tile([P, 512], U8, name="x_scales", align_bytes=64, bufs=4)
+            live["xq", s] = (codes, scales)
+            nc.vector.quantize_mx(out=codes[:].bitcast(FP8X4), scales=scales[:], in_=live["grouped", s][:].rearrange("p g n -> p (g n)"))
+
+        def features(s, b):
+            G, tp = b // 2, b % 2
+            bank = mps.tile([P, 2, 256], F32, name="bank")
+            live["h", s, b] = bank
+            codes, scales = live["xq", s]
+            for tt in range(2):
+                for g in range(2):
+                    nc.tensor.matmul_mx(
+                        out=bank[:, tt, :],
+                        lhsT=w_codes[g, G, tp][:, P * tt : P * (tt + 1)].bitcast(FP8X4),
+                        lhsT_scale=w_scales[g, G, tp][:, P * tt : P * (tt + 1)],
+                        rhs=codes[:, 256 * g : 256 * (g + 1)].bitcast(FP8X4),
+                        rhs_scale=scales[:, 256 * g : 256 * (g + 1)],
+                        start=(g == 0),
+                        stop=(g == 1),
+                    )
+
+        def relu_sum(s, b, eng):
+            bank = live["h", s, b][:].rearrange("p t n -> p (t n)")
+            total = acc2[s // 8, b // 2][:, 2 * (b % 2) : 2 * (b % 2) + 2, :].rearrange("p t n -> p (t n)")
+            if s % 8 == 0 and eng == "S":
+                nc.scalar.activation(out=total, in_=bank, func=ACT.Relu)
+            elif s % 8 == 0:
+                nc.vector.tensor_scalar(out=total, in0=bank, scalar1=0.0, scalar2=None, op0=ALU.max)
+            else:
+                nc.vector.scalar_tensor_tensor(out=total, in0=bank, scalar=0.0, in1=total, op0=ALU.max, op1=ALU.add)
+
+        def group_w(g, G, tp, eng):
+            grouped = work.tile([P, 2, P, 4], BF16, name="w_grouped", align_bytes=64, bufs=4)
+            live["wg", g, G, tp] = grouped
+            src = w_raw[g, G][:].rearrange("p j (m t) -> p t m j", t=4)[:, 2 * tp : 2 * tp + 2]
+            if eng == "S":
+                nc.scalar.copy(out=grouped[:], in_=src)
+            elif eng == "G":
+                nc.gpsimd.tensor_scalar(out=grouped[:], in0=src, scalar1=1.0, scalar2=0.0, op0=ALU.mult, op1=ALU.add)
+            else:
+                nc.vector.tensor_copy(out=grouped[:], in_=src)
+
+        def quant_w(g, G, tp):
+            nc.vector.quantize_mx(
+                out=w_codes[g, G, tp][:].bitcast(FP8X4),
+                scales=w_scales[g, G, tp][:],
+                in_=live["wg", g, G, tp][:].rearrange("p t m j -> p (t m j)"),
+            )
+
+        def group_a(h, G, c, eng):
+            if ("ag", h, G) not in live:
+                live["ag", h, G] = work.tile([P, 256, 4], BF16, name="a_grouped", align_bytes=64, bufs=2)
+            dst = live["ag", h, G][:, P * c : P * (c + 1), :]
+            src = acc2[h, G][:, :, P * c : P * (c + 1)].rearrange("p t n -> p n t")
+            if eng == "S":
+                nc.scalar.activation(out=dst, in_=src, func=ACT.Copy, scale=1.0 / C)
+            else:
+                nc.vector.tensor_scalar(out=dst, in0=src, scalar1=1.0 / C, scalar2=None, op0=ALU.mult)
+
+        def quant_a(h, G):
+            codes = work.tile([P, 256], U32, name="a_codes", align_bytes=64, bufs=4)
+            scales = work.tile([P, 256], U8, name="a_scales", align_bytes=64, bufs=4)
+            live["aq", h, G] = (codes, scales)
+            nc.vector.quantize_mx(out=codes[:].bitcast(FP8X4), scales=scales[:], in_=live["ag", h, G][:].rearrange("p n t -> p (n t)"))
+
+        def scores(h, qp):
+            bank = mps.tile([P, 2, 256], F32, name="bank")
+            live["z", h, qp] = bank
+            for qq in range(2):
+                qt = 2 * qp + qq
+                for c in range(2):
+                    for g in range(2):
+                        codes, scales = live["aq", h, g]
+                        nc.tensor.matmul_mx(
+                            out=bank[:, qq, P * c : P * (c + 1)],
+                            lhsT=q_words[:, g, 2 * P * qt : 2 * P * (qt + 1)].bitcast(FP4X4),
+                            lhsT_scale=q_scales[:, g, P * qt : P * (qt + 1)],
+                            rhs=codes[:, P * c : P * (c + 1)].bitcast(FP8X4),
+                            rhs_scale=scales[:, P * c : P * (c + 1)],
+                            start=(g == 0),
+                            stop=(g == 1),
+                        )
+
+        def expo(h, qp):
+            e = work.tile([P, 2, 256], F32, name="expo", bufs=4)
+            live["e", h, qp] = e
+            nc.scalar.activation(out=e[:], in_=live["z", h, qp][:], func=ACT.Exp)
+
+        def masked(h, qp, eng):
+            e = live["e", h, qp]
+            engine = nc.vector if eng == "V" else nc.gpsimd
+            engine.tensor_tensor(out=e[:], in0=e[:], in1=mask_sb[:, 2 * qp : 2 * qp + 2, 256 * h : 256 * (h + 1)], op=ALU.mult)
+
+        def store(h, qp):
+            nc.sync.dma_start(out=out_view[:, 2 * qp : 2 * qp + 2, 256 * h : 256 * (h + 1)], in_=live["e", h, qp][:])
+
+        for task in build_order():
+            kind = task[0]
+            if kind == "L":
+                load(task[1])
+            elif kind == "WV":
+                widen_split(task[1], task[2], task[3])
+            elif kind == "WS":
+                widen_plain(wide_tile(task[1], 1, task[2]), task[1], 1, task[2], task[3])
+            else:
+                {"T": turn, "C": copy_out, "Q": quant_x, "M": features, "R": relu_sum, "WI": group_w, "WQ": quant_w,
+                 "AI": group_a, "AQ": quant_a, "Z": scores, "E": expo, "K": masked, "ST": store}[kind](*task[1:])

@@ -18,38 +18,8 @@ T, K, N, M, C = 4096, 1024, 1024, 1024, 8
 P = 128
 FLOPS = 2 * T * K * N + 2 * M * N * (T // C)
 
-
 def build_order():
-    o=[]
-    o+=[('L','xs0',64),('L','x0',256),('L','w00',512),('L','w10',512),('L','x1',256),('L','x2',256),('L','w01',512),('L','w11',512),('L','x3',256),('L','x4',256),('L','xs1',64)]
-    o+=[('L','x%d'%s,256) for s in range(5,8)]+[('L','q',600),('L','mask',1024)]+[('L','x%d'%s,256) for s in range(8,16)]
-    V,S='V','S'
-    o+=[('WV',0,0,V),('WV',0,1,V),('WS',0,0,S),('WS',0,1,V),('T',0,0),('T',0,1)]
-    o+=[('WI',0,0,0,V),('C',0,0,S),('C',0,1,S),('WI',0,0,1,V),('WI',1,0,0,V),('WQ',0,0,0),('WQ',0,0,1),('WQ',1,0,0),('Q',0),('WS',1,0,S),('WS',1,1,S),('WI',1,0,1,V),('WV',1,0,V),('WV',1,1,V),('WQ',1,0,1),('WV',2,0,V),('WV',2,1,V)]
-    o+=[('M',0,0),('T',1,0),('T',1,1),('M',0,1),('WS',2,0,S),('C',1,0,S),('C',1,1,S),('WI',0,1,0,V),('WS',2,1,S),('WI',1,1,0,V),('WQ',0,1,0),('Q',1),('WQ',1,1,0),('R',0,0,S),('R',0,1,S),('T',2,0),('T',2,1),('M',1,0),('M',1,1),('WI',0,1,1,V),('C',2,0,S),('C',2,1,S),('WI',1,1,1,V),('WQ',0,1,1),('WV',3,0,V),('WQ',1,1,1),('M',0,2),('M',0,3),('WS',3,0,S),('WS',3,1,S),('WV',3,1,V),('R',1,0,V),('Q',2),('R',0,2,S),('R',0,3,S),('R',1,1,V),('M',1,2),('M',1,3),('WS',4,0,S),('WS',4,1,S),('WV',4,0,V),('WV',4,1,V)]
-    pend=[('R',1,2,V),('R',1,3,V)]
-    for i in range(2,14):
-        first = i==8
-        n=i+3
-        o+=[('T',i+1,0),('T',i+1,1)]
-        o+=pend; pend=[]
-        o+=[('C',i+1,0,S),('C',i+1,1,S)]
-        if first:
-            o+=[('WV',n,0,V),('WV',n,1,V),('WS',n,0,V),('Q',i+1),('WS',n,1,V),('AI',0,0,0,V),('AI',0,0,1,V),('AI',0,1,0,V),('AQ',0,0),('AI',0,1,1,V),('WV',n+1,0,V),('AQ',0,1)]
-            o+=[('M',i,0),('R',i,0,S),('M',i,1),('R',i,1,S),('M',i,2),('R',i,2,S),('M',i,3),('R',i,3,S)]
-            continue
-        if n<16:
-            if i!=9: o+=[('WV',n,0,V)]
-            o+=[('WS',n,0,S),('WS',n,1,S),('WV',n,1,S if SW(i) else V)]
-        o+=[('M',i,0),('R',i,0,V),('M',i,1),('R',i,1,V),('Q',i+1),('M',i,2),('R',i,2,V),('M',i,3)]
-        pend=[('R',i,3,V)]
-        if 9<=i<=12:
-            o+=[('Z',0,i-9),('E',0,i-9)]; pend+=[('K',0,i-9,V),('ST',0,i-9)]
-    o+=[('T',15,0),('T',15,1)]+pend+[('C',15,0,S),('C',15,1,S),('M',14,0),('M',14,1),('R',14,0,V),('Q',15),('R',14,1,V),('M',14,2),('M',15,0),('M',15,1),('M',14,3),('M',15,2),('M',15,3)]
-    o+=[('R',14,2,V),('R',15,0,V),('R',15,1,V),('R',14,3,V),('AI',1,0,0,S),('AI',1,0,1,S),('R',15,2,V),('R',15,3,V),('AQ',1,0),('AI',1,1,0,V),('AI',1,1,1,S),('AQ',1,1)]
-    for q in range(4): o+=[('Z',1,q),('E',1,q),('K',1,q,V),('ST',1,q)]
-    return o
-def SW(i): return i<8 or i>9
+    return [('L', 'x0', 256), ('L', 'xs0', 64), ('L', 'x1', 256), ('L', 'x2', 256), ('L', 'w00', 512), ('L', 'x3', 256), ('L', 'w10', 512), ('L', 'x5', 256), ('L', 'w11', 512), ('L', 'x4', 256), ('L', 'w01', 512), ('L', 'xs1', 64), ('L', 'x6', 256), ('L', 'x7', 256), ('L', 'x8', 256), ('L', 'x9', 256), ('L', 'q', 600), ('L', 'mask', 1024), ('L', 'x10', 256), ('L', 'x11', 256), ('L', 'x12', 256), ('L', 'x13', 256), ('L', 'x14', 256), ('L', 'x15', 256), ('W', 0, 1, 0, 'V'), ('W', 0, 1, 1, 'V'), ('W', 1, 0, 0, 'V'), ('W', 0, 0, 1, 'S'), ('W', 0, 0, 0, 'S'), ('W', 1, 1, 0, 'S'), ('W', 1, 1, 1, 'V'), ('T', 0, 0), ('W', 2, 0, 1, 'V'), ('W', 2, 0, 0, 'V'), ('W', 1, 0, 1, 'S'), ('T', 0, 1), ('WI', 0, 0, 0, 'V'), ('T', 1, 0), ('C', 0, 0, 'S'), ('C', 0, 1, 'S'), ('T', 1, 1), ('T', 2, 0), ('WI', 0, 0, 1, 'V'), ('W', 2, 1, 1, 'S'), ('C', 1, 0, 'S'), ('WI', 1, 0, 1, 'V'), ('C', 1, 1, 'S'), ('WI', 1, 0, 0, 'V'), ('Q', 0), ('W', 2, 1, 0, 'S'), ('WQ', 0, 0, 0), ('C', 2, 0, 'S'), ('WQ', 1, 0, 0), ('W', 3, 1, 1, 'V'), ('T', 2, 1), ('WQ', 0, 0, 1), ('WQ', 1, 0, 1), ('Q', 1), ('W', 3, 1, 0, 'S'), ('M', 0, 1), ('M', 0, 0), ('M', 1, 0), ('T', 3, 1), ('C', 2, 1, 'S'), ('W', 3, 0, 1, 'S'), ('WI', 1, 1, 0, 'V'), ('M', 1, 1), ('R', 0, 1, 'S'), ('W', 3, 0, 0, 'S'), ('Q', 2), ('R', 0, 0, 'S'), ('WI', 0, 1, 0, 'V'), ('WQ', 1, 1, 0), ('W', 5, 1, 1, 'V'), ('WQ', 0, 1, 0), ('WI', 1, 1, 1, 'S'), ('T', 3, 0), ('WI', 0, 1, 1, 'V'), ('R', 1, 0, 'V'), ('M', 0, 2), ('WQ', 1, 1, 1), ('M', 1, 2), ('WQ', 0, 1, 1), ('W', 4, 1, 1, 'S'), ('R', 1, 1, 'V'), ('W', 4, 0, 1, 'V'), ('R', 0, 2, 'S'), ('M', 2, 0), ('R', 1, 2, 'V'), ('M', 2, 1), ('W', 4, 1, 0, 'V'), ('M', 0, 3), ('M', 2, 2), ('M', 1, 3), ('C', 3, 1, 'S'), ('W', 4, 0, 0, 'S'), ('M', 2, 3), ('R', 2, 0, 'V'), ('C', 3, 0, 'S'), ('R', 0, 3, 'S'), ('Q', 3), ('R', 1, 3, 'V'), ('W', 5, 0, 0, 'S'), ('R', 2, 1, 'V'), ('W', 5, 1, 0, 'S'), ('W', 5, 0, 1, 'S'), ('R', 2, 2, 'V'), ('T', 4, 0), ('T', 4, 1), ('R', 2, 3, 'V'), ('C', 4, 0, 'S'), ('C', 4, 1, 'S'), ('W', 6, 0, 0, 'S'), ('W', 6, 0, 1, 'S'), ('W', 6, 1, 0, 'S'), ('W', 6, 1, 1, 'S'), ('M', 3, 0), ('R', 3, 0, 'V'), ('M', 3, 1), ('R', 3, 1, 'V'), ('Q', 4), ('M', 3, 2), ('R', 3, 2, 'V'), ('M', 3, 3), ('T', 5, 0), ('T', 5, 1), ('R', 3, 3, 'V'), ('C', 5, 0, 'S'), ('C', 5, 1, 'S'), ('W', 7, 0, 0, 'V'), ('W', 7, 0, 1, 'S'), ('W', 7, 1, 0, 'S'), ('W', 7, 1, 1, 'S'), ('M', 4, 0), ('R', 4, 0, 'V'), ('M', 4, 1), ('R', 4, 1, 'V'), ('Q', 5), ('M', 4, 2), ('R', 4, 2, 'V'), ('M', 4, 3), ('T', 6, 0), ('T', 6, 1), ('R', 4, 3, 'V'), ('C', 6, 0, 'S'), ('C', 6, 1, 'S'), ('W', 8, 0, 0, 'V'), ('W', 8, 0, 1, 'S'), ('W', 8, 1, 0, 'S'), ('W', 8, 1, 1, 'S'), ('M', 5, 0), ('R', 5, 0, 'V'), ('M', 5, 1), ('R', 5, 1, 'V'), ('Q', 6), ('M', 5, 2), ('R', 5, 2, 'V'), ('M', 5, 3), ('T', 7, 0), ('T', 7, 1), ('R', 5, 3, 'V'), ('C', 7, 0, 'S'), ('C', 7, 1, 'S'), ('W', 9, 0, 0, 'V'), ('W', 9, 0, 1, 'S'), ('W', 9, 1, 0, 'S'), ('W', 9, 1, 1, 'S'), ('M', 6, 0), ('R', 6, 0, 'V'), ('M', 6, 1), ('R', 6, 1, 'V'), ('Q', 7), ('M', 6, 2), ('R', 6, 2, 'V'), ('M', 6, 3), ('T', 8, 0), ('T', 8, 1), ('R', 6, 3, 'V'), ('C', 8, 0, 'S'), ('C', 8, 1, 'S'), ('W', 10, 0, 0, 'V'), ('W', 10, 0, 1, 'S'), ('W', 10, 1, 0, 'S'), ('W', 10, 1, 1, 'S'), ('M', 7, 0), ('R', 7, 0, 'V'), ('M', 7, 1), ('R', 7, 1, 'V'), ('AQ', 0, 0), ('Q', 8), ('AQ', 0, 1), ('M', 7, 2), ('R', 7, 2, 'V'), ('M', 7, 3), ('T', 9, 0), ('T', 9, 1), ('R', 7, 3, 'V'), ('AQ', 0, 2), ('C', 9, 0, 'S'), ('C', 9, 1, 'S'), ('Q', 9), ('AQ', 0, 3), ('W', 11, 0, 0, 'V'), ('W', 11, 0, 1, 'V'), ('W', 11, 1, 0, 'V'), ('W', 11, 1, 1, 'V'), ('M', 8, 0), ('R', 8, 0, 'S'), ('M', 8, 1), ('R', 8, 1, 'S'), ('M', 8, 2), ('R', 8, 2, 'S'), ('M', 8, 3), ('T', 10, 0), ('T', 10, 1), ('R', 8, 3, 'S'), ('C', 10, 0, 'S'), ('C', 10, 1, 'S'), ('W', 12, 0, 0, 'V'), ('W', 12, 0, 1, 'V'), ('W', 12, 1, 0, 'S'), ('W', 12, 1, 1, 'S'), ('M', 9, 0), ('R', 9, 0, 'V'), ('M', 9, 1), ('R', 9, 1, 'V'), ('Q', 10), ('M', 9, 2), ('R', 9, 2, 'V'), ('M', 9, 3), ('Z', 0, 0), ('E', 0, 0), ('T', 11, 0), ('T', 11, 1), ('R', 9, 3, 'V'), ('C', 11, 0, 'S'), ('C', 11, 1, 'S'), ('W', 13, 0, 0, 'V'), ('W', 13, 0, 1, 'S'), ('W', 13, 1, 0, 'S'), ('W', 13, 1, 1, 'S'), ('M', 10, 0), ('R', 10, 0, 'V'), ('M', 10, 1), ('R', 10, 1, 'V'), ('Q', 11), ('M', 10, 2), ('R', 10, 2, 'V'), ('M', 10, 3), ('Z', 0, 1), ('E', 0, 1), ('T', 12, 0), ('T', 12, 1), ('R', 10, 3, 'V'), ('K', 0, 0, 'V'), ('ST', 0, 0), ('C', 12, 0, 'S'), ('C', 12, 1, 'S'), ('W', 14, 0, 0, 'V'), ('W', 14, 0, 1, 'V'), ('W', 14, 1, 0, 'V'), ('W', 14, 1, 1, 'S'), ('M', 11, 0), ('R', 11, 0, 'V'), ('M', 11, 1), ('R', 11, 1, 'V'), ('Q', 12), ('M', 11, 2), ('R', 11, 2, 'V'), ('M', 11, 3), ('Z', 0, 2), ('E', 0, 2), ('T', 13, 0), ('T', 13, 1), ('R', 11, 3, 'V'), ('K', 0, 1, 'V'), ('ST', 0, 1), ('C', 13, 0, 'S'), ('C', 13, 1, 'S'), ('W', 15, 0, 0, 'V'), ('W', 15, 0, 1, 'S'), ('W', 15, 1, 0, 'S'), ('W', 15, 1, 1, 'S'), ('M', 12, 0), ('R', 12, 0, 'V'), ('M', 12, 1), ('R', 12, 1, 'V'), ('Q', 13), ('M', 12, 2), ('R', 12, 2, 'V'), ('M', 12, 3), ('Z', 0, 3), ('E', 0, 3), ('T', 14, 0), ('T', 14, 1), ('R', 12, 3, 'V'), ('K', 0, 2, 'V'), ('ST', 0, 2), ('C', 14, 0, 'S'), ('C', 14, 1, 'S'), ('M', 13, 0), ('R', 13, 0, 'V'), ('M', 13, 1), ('R', 13, 1, 'V'), ('Q', 14), ('M', 13, 2), ('R', 13, 2, 'V'), ('M', 13, 3), ('T', 15, 0), ('T', 15, 1), ('R', 13, 3, 'V'), ('K', 0, 3, 'V'), ('ST', 0, 3), ('C', 15, 0, 'S'), ('C', 15, 1, 'S'), ('M', 14, 0), ('R', 14, 0, 'V'), ('M', 14, 1), ('R', 14, 1, 'V'), ('Q', 15), ('M', 14, 2), ('R', 14, 2, 'V'), ('M', 14, 3), ('R', 14, 3, 'V'), ('M', 15, 0), ('R', 15, 0, 'V'), ('M', 15, 1), ('R', 15, 1, 'V'), ('AQ', 1, 0), ('M', 15, 2), ('R', 15, 2, 'V'), ('AQ', 1, 1), ('M', 15, 3), ('Z', 1, 0), ('R', 15, 3, 'V'), ('AQ', 1, 2), ('Z', 1, 1), ('E', 1, 0), ('AQ', 1, 3), ('K', 1, 0, 'V'), ('ST', 1, 0), ('E', 1, 1), ('K', 1, 1, 'V'), ('ST', 1, 1), ('Z', 1, 2), ('E', 1, 2), ('K', 1, 2, 'V'), ('ST', 1, 2), ('Z', 1, 3), ('E', 1, 3, 0, 2), ('E', 1, 3, 2, 4), ('K', 1, 3, 'V', 0, 2), ('ST', 1, 3, 0, 2), ('K', 1, 3, 'V', 2, 4), ('ST', 1, 3, 2, 4)]
 
 
 def tile_masked_block_scores_d4_kernel(tc, x_bytes, x_scale, w, query_words, query_scales, mask, out):
@@ -98,12 +68,7 @@ def tile_masked_block_scores_d4_kernel(tc, x_bytes, x_scale, w, query_words, que
             elif name.startswith("w"):
                 g, G = int(name[1]), int(name[2])
                 rows = w[512 * g : 512 * (g + 1), 512 * G : 512 * (G + 1)]
-                if g == 0:
-                    by_half = rows.rearrange("(b u r) n -> u b r n", u=2, r=16)
-                    for u in range(2):
-                        nc.sync.dma_start(out=w_raw[g, G][:, 2 * u : 2 * u + 2, :], in_=by_half[u])
-                else:
-                    nc.sync.dma_start(out=w_raw[g, G][:], in_=rows.rearrange("(p j) n -> p j n", j=4))
+                nc.sync.dma_start(out=w_raw[g, G][:], in_=rows.rearrange("(p j) n -> p j n", j=4))
             elif name == "q":
                 for quad in range(4):
                     nc.sync.dma_start(
@@ -115,10 +80,13 @@ def tile_masked_block_scores_d4_kernel(tc, x_bytes, x_scale, w, query_words, que
                 nc.sync.dma_start(out=mask_sb[:], in_=mask.rearrange("(t p) b -> p t b", p=P))
 
         def wide_tile(s, g, c):
-            live["wide", s, g, c] = work.tile([P, 512], BF16, name="wide%d%d" % (g, c), bufs=4)
+            live["wide", s, g, c] = work.tile([P, 512], BF16, name="wide%d%d" % (g, c), bufs=6)
             return live["wide", s, g, c]
 
-        def widen_plain(dst, s, g, c, eng):
+        def widen(s, g, c, eng):
+            dst = wide_tile(s, g, c)
+            live["split", s, g, c] = eng == "V"
+            halves = dst[:].rearrange("p (u w e) -> p w u e", u=2, e=2)
             for q in range(4):
                 blk = 4 * g + q
                 src = xb[s][:, c, P * blk : P * (blk + 1)].bitcast(FP8)
@@ -126,23 +94,11 @@ def tile_masked_block_scores_d4_kernel(tc, x_bytes, x_scale, w, query_words, que
                 if eng == "S":
                     nc.scalar.activation(out=dst[:, P * q : P * (q + 1)], in_=src, func=ACT.Copy, scale=scale)
                 else:
-                    nc.vector.tensor_scalar(out=dst[:, P * q : P * (q + 1)], in0=src, scalar1=scale, scalar2=None, op0=ALU.mult)
-
-        def widen_split(s, c, eng):
-            dst = wide_tile(s, 0, c)
-            if eng == "S":
-                plain = work.tile([P, 512], BF16, name="plain", bufs=2)
-                widen_plain(plain, s, 0, c, "S")
-                nc.scalar.copy(
-                    out=dst[:].rearrange("p (u b e) -> p u b e", u=2, e=16),
-                    in_=plain[:].rearrange("p (b u e) -> p u b e", u=2, e=16),
-                )
-                return
-            halves = dst[:].rearrange("p (u b e) -> p b u e", u=2, e=16)
-            for q in range(4):
-                src = xb[s][:, c, P * q : P * (q + 1)].bitcast(FP8).rearrange("p (b u e) -> p b u e", u=2, e=16)
-                scale = xs[s // 8][:, c, 8 * (s % 8) + q : 8 * (s % 8) + q + 1]
-                nc.vector.tensor_scalar(out=halves[:, 4 * q : 4 * q + 4], in0=src, scalar1=scale, scalar2=None, op0=ALU.mult)
+                    nc.vector.tensor_scalar(
+                        out=halves[:, 32 * q : 32 * (q + 1)],
+                        in0=src.rearrange("p (w u e) -> p w u e", u=2, e=2),
+                        scalar1=scale, scalar2=None, op0=ALU.mult,
+                    )
 
         def turn(s, g):
             bank = tps.tile([P, 2, 2, P], F32, name="turned%d" % g)
@@ -150,11 +106,11 @@ def tile_masked_block_scores_d4_kernel(tc, x_bytes, x_scale, w, query_words, que
             for c in range(2):
                 words = live["wide", s, g, c][:].bitcast(F32)
                 for u in range(2):
-                    src = words[:, P * u : P * (u + 1)] if g == 0 else words[:, u : 2 * P : 2]
+                    src = words[:, P * u : P * (u + 1)] if live["split", s, g, c] else words[:, u : 2 * P : 2]
                     nc.tensor.transpose(bank[:, c, u, :], src, ident[:])
 
         def copy_out(s, g, eng):
-            if g == 0:
+            if ("grouped", s) not in live:
                 live["grouped", s] = work.tile([P, 2, 1024], BF16, name="x_grouped", align_bytes=64)
             dst = live["grouped", s][:, g, :].bitcast(F32).rearrange("p (c r u) -> p c r u", c=2, u=2)
             src = live["turned", s, g][:].rearrange("p c u r -> p c r u")
@@ -174,6 +130,22 @@ def tile_masked_block_scores_d4_kernel(tc, x_bytes, x_scale, w, query_words, que
             bank = mps.tile([P, 2, 256], F32, name="bank")
             live["h", s, b] = bank
             codes, scales = live["xq", s]
+            if s % 8 == 7:
+                c, G = b // 2, b % 2
+                quarters = bank[:].rearrange("p a (b n) -> p (a b) n", n=P)
+                for t in range(4):
+                    for g in range(2):
+                        cols = slice(256 * g + P * c, 256 * g + P * (c + 1))
+                        nc.tensor.matmul_mx(
+                            out=quarters[:, t, :],
+                            lhsT=w_codes[g, G, t // 2][:, P * (t % 2) : P * (t % 2 + 1)].bitcast(FP8X4),
+                            lhsT_scale=w_scales[g, G, t // 2][:, P * (t % 2) : P * (t % 2 + 1)],
+                            rhs=codes[:, cols].bitcast(FP8X4),
+                            rhs_scale=scales[:, cols],
+                            start=(g == 0),
+                            stop=(g == 1),
+                        )
+                return
             for tt in range(2):
                 for g in range(2):
                     nc.tensor.matmul_mx(
@@ -187,6 +159,19 @@ def tile_masked_block_scores_d4_kernel(tc, x_bytes, x_scale, w, query_words, que
                     )
 
         def relu_sum(s, b, eng):
+            if s % 8 == 7:
+                c, G = b // 2, b % 2
+                grouped = work.tile([P, P, 4], BF16, name="a_grouped", align_bytes=64, bufs=4)
+                live["ag", s // 8, b] = grouped
+                nc.vector.scalar_tensor_tensor(
+                    out=grouped[:],
+                    in0=live["h", s, b][:].rearrange("p a (b n) -> p n (a b)", n=P),
+                    scalar=0.0,
+                    in1=acc2[s // 8, G][:, :, P * c : P * (c + 1)].rearrange("p t n -> p n t"),
+                    op0=ALU.max,
+                    op1=ALU.add,
+                )
+                return
             bank = live["h", s, b][:].rearrange("p t n -> p (t n)")
             total = acc2[s // 8, b // 2][:, 2 * (b % 2) : 2 * (b % 2) + 2, :].rearrange("p t n -> p (t n)")
             if s % 8 == 0 and eng == "S":
@@ -214,61 +199,55 @@ def tile_masked_block_scores_d4_kernel(tc, x_bytes, x_scale, w, query_words, que
                 in_=live["wg", g, G, tp][:].rearrange("p t m j -> p (t m j)"),
             )
 
-        def group_a(h, G, c, eng):
-            if ("ag", h, G) not in live:
-                live["ag", h, G] = work.tile([P, 256, 4], BF16, name="a_grouped", align_bytes=64, bufs=2)
-            dst = live["ag", h, G][:, P * c : P * (c + 1), :]
-            src = acc2[h, G][:, :, P * c : P * (c + 1)].rearrange("p t n -> p n t")
-            if eng == "S":
-                nc.scalar.activation(out=dst, in_=src, func=ACT.Copy, scale=1.0 / C)
-            else:
-                nc.vector.tensor_scalar(out=dst, in0=src, scalar1=1.0 / C, scalar2=None, op0=ALU.mult)
+        def quant_a(h, b):
+            codes = work.tile([P, P], U32, name="a_codes", align_bytes=64, bufs=8)
+            scales = work.tile([P, P], U8, name="a_scales", align_bytes=64, bufs=8)
+            live["aq", h, b] = (codes, scales)
+            nc.vector.quantize_mx(out=codes[:].bitcast(FP8X4), scales=scales[:], in_=live["ag", h, b][:].rearrange("p n t -> p (n t)"))
 
-        def quant_a(h, G):
-            codes = work.tile([P, 256], U32, name="a_codes", align_bytes=64, bufs=4)
-            scales = work.tile([P, 256], U8, name="a_scales", align_bytes=64, bufs=4)
-            live["aq", h, G] = (codes, scales)
-            nc.vector.quantize_mx(out=codes[:].bitcast(FP8X4), scales=scales[:], in_=live["ag", h, G][:].rearrange("p n t -> p (n t)"))
+        def scores(h, b):
+            c, qh = b // 2, b % 2
+            bank = mps.tile([P, 4, P], F32, name="bank")
+            live["z", h, b] = bank
+            for qq in range(4):
+                qt = 4 * qh + qq
+                for g in range(2):
+                    codes, scales = live["aq", h, 2 * c + g]
+                    nc.tensor.matmul_mx(
+                        out=bank[:, qq, :],
+                        lhsT=q_words[:, g, 2 * P * qt : 2 * P * (qt + 1)].bitcast(FP4X4),
+                        lhsT_scale=q_scales[:, g, P * qt : P * (qt + 1)],
+                        rhs=codes[:].bitcast(FP8X4),
+                        rhs_scale=scales[:],
+                        start=(g == 0),
+                        stop=(g == 1),
+                    )
 
-        def scores(h, qp):
-            bank = mps.tile([P, 2, 256], F32, name="bank")
-            live["z", h, qp] = bank
-            for qq in range(2):
-                qt = 2 * qp + qq
-                for c in range(2):
-                    for g in range(2):
-                        codes, scales = live["aq", h, g]
-                        nc.tensor.matmul_mx(
-                            out=bank[:, qq, P * c : P * (c + 1)],
-                            lhsT=q_words[:, g, 2 * P * qt : 2 * P * (qt + 1)].bitcast(FP4X4),
-                            lhsT_scale=q_scales[:, g, P * qt : P * (qt + 1)],
-                            rhs=codes[:, P * c : P * (c + 1)].bitcast(FP8X4),
-                            rhs_scale=scales[:, P * c : P * (c + 1)],
-                            start=(g == 0),
-                            stop=(g == 1),
-                        )
+        def window(h, b, lo, hi):
+            c, qh = b // 2, b % 2
+            return slice(4 * qh + lo, 4 * qh + hi), slice(256 * h + P * c, 256 * h + P * (c + 1))
 
-        def expo(h, qp):
-            e = work.tile([P, 2, 256], F32, name="expo", bufs=4)
-            live["e", h, qp] = e
-            nc.scalar.activation(out=e[:], in_=live["z", h, qp][:], func=ACT.Exp)
+        def expo(h, b, lo=0, hi=4):
+            e = work.tile([P, hi - lo, P], F32, name="expo", bufs=4)
+            live["e", h, b, lo] = e
+            nc.scalar.activation(out=e[:], in_=live["z", h, b][:, lo:hi, :], func=ACT.Exp, scale=1.0 / C)
 
-        def masked(h, qp, eng):
-            e = live["e", h, qp]
+        def masked(h, b, eng, lo=0, hi=4):
+            e = live["e", h, b, lo]
+            rows, cols = window(h, b, lo, hi)
             engine = nc.vector if eng == "V" else nc.gpsimd
-            engine.tensor_tensor(out=e[:], in0=e[:], in1=mask_sb[:, 2 * qp : 2 * qp + 2, 256 * h : 256 * (h + 1)], op=ALU.mult)
+            engine.tensor_tensor(out=e[:], in0=e[:], in1=mask_sb[:, rows, cols], op=ALU.mult)
 
-        def store(h, qp):
-            nc.sync.dma_start(out=out_view[:, 2 * qp : 2 * qp + 2, 256 * h : 256 * (h + 1)], in_=live["e", h, qp][:])
+        def store(h, b, lo=0, hi=4):
+            rows, cols = window(h, b, lo, hi)
+            nc.sync.dma_start(out=out_view[:, rows, cols], in_=live["e", h, b, lo][:])
 
         for task in build_order():
             kind = task[0]
             if kind == "L":
                 load(task[1])
-            elif kind == "WV":
-                widen_split(task[1], task[2], task[3])
-            elif kind == "WS":
-                widen_plain(wide_tile(task[1], 1, task[2]), task[1], 1, task[2], task[3])
+            elif kind == "W":
+                widen(*task[1:])
             else:
                 {"T": turn, "C": copy_out, "Q": quant_x, "M": features, "R": relu_sum, "WI": group_w, "WQ": quant_w,
-                 "AI": group_a, "AQ": quant_a, "Z": scores, "E": expo, "K": masked, "ST": store}[kind](*task[1:])
+                 "AQ": quant_a, "Z": scores, "E": expo, "K": masked, "ST": store}[kind](*task[1:])

@@ -19,7 +19,12 @@ P = 128
 FLOPS = 2 * T * K * N + 2 * M * N * (T // C)
 
 def build_order():
-    return [('L', 'x0', 256), ('L', 'xs0', 64), ('L', 'x1', 256), ('L', 'x2', 256), ('L', 'w00', 512), ('L', 'x3', 256), ('L', 'w10', 512), ('L', 'x5', 256), ('L', 'w11', 512), ('L', 'x4', 256), ('L', 'w01', 512), ('L', 'xs1', 64), ('L', 'x6', 256), ('L', 'x7', 256), ('L', 'x8', 256), ('L', 'x9', 256), ('L', 'q', 600), ('L', 'mask', 1024), ('L', 'x10', 256), ('L', 'x11', 256), ('L', 'x12', 256), ('L', 'x13', 256), ('L', 'x14', 256), ('L', 'x15', 256), ('W', 0, 1, 0, 'V'), ('W', 0, 1, 1, 'V'), ('W', 1, 0, 0, 'V'), ('W', 0, 0, 1, 'S'), ('W', 0, 0, 0, 'S'), ('W', 1, 1, 0, 'S'), ('W', 1, 1, 1, 'V'), ('T', 0, 0), ('W', 2, 0, 1, 'V'), ('W', 2, 0, 0, 'V'), ('W', 1, 0, 1, 'S'), ('T', 0, 1), ('WI', 0, 0, 0, 'V'), ('T', 1, 0), ('C', 0, 0, 'S'), ('C', 0, 1, 'S'), ('T', 1, 1), ('T', 2, 0), ('WI', 0, 0, 1, 'V'), ('W', 2, 1, 1, 'S'), ('C', 1, 0, 'S'), ('WI', 1, 0, 1, 'V'), ('C', 1, 1, 'S'), ('WI', 1, 0, 0, 'V'), ('Q', 0), ('W', 2, 1, 0, 'S'), ('WQ', 0, 0, 0), ('C', 2, 0, 'S'), ('WQ', 1, 0, 0), ('W', 3, 1, 1, 'V'), ('T', 2, 1), ('WQ', 0, 0, 1), ('WQ', 1, 0, 1), ('Q', 1), ('W', 3, 1, 0, 'S'), ('M', 0, 1), ('M', 0, 0), ('M', 1, 0), ('T', 3, 1), ('C', 2, 1, 'S'), ('W', 3, 0, 1, 'S'), ('WI', 1, 1, 0, 'V'), ('M', 1, 1), ('R', 0, 1, 'S'), ('W', 3, 0, 0, 'S'), ('Q', 2), ('R', 0, 0, 'S'), ('WI', 0, 1, 0, 'V'), ('WQ', 1, 1, 0), ('W', 5, 1, 1, 'V'), ('WQ', 0, 1, 0), ('WI', 1, 1, 1, 'S'), ('T', 3, 0), ('WI', 0, 1, 1, 'V'), ('R', 1, 0, 'V'), ('M', 0, 2), ('WQ', 1, 1, 1), ('M', 1, 2), ('WQ', 0, 1, 1), ('W', 4, 1, 1, 'S'), ('R', 1, 1, 'V'), ('W', 4, 0, 1, 'V'), ('R', 0, 2, 'S'), ('M', 2, 0), ('R', 1, 2, 'V'), ('M', 2, 1), ('W', 4, 1, 0, 'V'), ('M', 0, 3), ('M', 2, 2), ('M', 1, 3), ('C', 3, 1, 'S'), ('W', 4, 0, 0, 'S'), ('M', 2, 3), ('R', 2, 0, 'V'), ('C', 3, 0, 'S'), ('R', 0, 3, 'S'), ('Q', 3), ('R', 1, 3, 'V'), ('W', 5, 0, 0, 'S'), ('R', 2, 1, 'V'), ('W', 5, 1, 0, 'S'), ('W', 5, 0, 1, 'S'), ('R', 2, 2, 'V'), ('T', 4, 0), ('T', 4, 1), ('R', 2, 3, 'V'), ('C', 4, 0, 'S'), ('C', 4, 1, 'S'), ('W', 6, 0, 0, 'S'), ('W', 6, 0, 1, 'S'), ('W', 6, 1, 0, 'S'), ('W', 6, 1, 1, 'S'), ('M', 3, 0), ('R', 3, 0, 'V'), ('M', 3, 1), ('R', 3, 1, 'V'), ('Q', 4), ('M', 3, 2), ('R', 3, 2, 'V'), ('M', 3, 3), ('T', 5, 0), ('T', 5, 1), ('R', 3, 3, 'V'), ('C', 5, 0, 'S'), ('C', 5, 1, 'S'), ('W', 7, 0, 0, 'V'), ('W', 7, 0, 1, 'S'), ('W', 7, 1, 0, 'S'), ('W', 7, 1, 1, 'S'), ('M', 4, 0), ('R', 4, 0, 'V'), ('M', 4, 1), ('R', 4, 1, 'V'), ('Q', 5), ('M', 4, 2), ('R', 4, 2, 'V'), ('M', 4, 3), ('T', 6, 0), ('T', 6, 1), ('R', 4, 3, 'V'), ('C', 6, 0, 'S'), ('C', 6, 1, 'S'), ('W', 8, 0, 0, 'V'), ('W', 8, 0, 1, 'S'), ('W', 8, 1, 0, 'S'), ('W', 8, 1, 1, 'S'), ('M', 5, 0), ('R', 5, 0, 'V'), ('M', 5, 1), ('R', 5, 1, 'V'), ('Q', 6), ('M', 5, 2), ('R', 5, 2, 'V'), ('M', 5, 3), ('T', 7, 0), ('T', 7, 1), ('R', 5, 3, 'V'), ('C', 7, 0, 'S'), ('C', 7, 1, 'S'), ('W', 9, 0, 0, 'V'), ('W', 9, 0, 1, 'S'), ('W', 9, 1, 0, 'S'), ('W', 9, 1, 1, 'S'), ('M', 6, 0), ('R', 6, 0, 'V'), ('M', 6, 1), ('R', 6, 1, 'V'), ('Q', 7), ('M', 6, 2), ('R', 6, 2, 'V'), ('M', 6, 3), ('T', 8, 0), ('T', 8, 1), ('R', 6, 3, 'V'), ('C', 8, 0, 'S'), ('C', 8, 1, 'S'), ('W', 10, 0, 0, 'V'), ('W', 10, 0, 1, 'S'), ('W', 10, 1, 0, 'S'), ('W', 10, 1, 1, 'S'), ('M', 7, 0), ('R', 7, 0, 'V'), ('M', 7, 1), ('R', 7, 1, 'V'), ('AQ', 0, 0), ('Q', 8), ('AQ', 0, 1), ('M', 7, 2), ('R', 7, 2, 'V'), ('M', 7, 3), ('T', 9, 0), ('T', 9, 1), ('R', 7, 3, 'V'), ('AQ', 0, 2), ('C', 9, 0, 'S'), ('C', 9, 1, 'S'), ('Q', 9), ('AQ', 0, 3), ('W', 11, 0, 0, 'V'), ('W', 11, 0, 1, 'V'), ('W', 11, 1, 0, 'V'), ('W', 11, 1, 1, 'V'), ('M', 8, 0), ('R', 8, 0, 'S'), ('M', 8, 1), ('R', 8, 1, 'S'), ('M', 8, 2), ('R', 8, 2, 'S'), ('M', 8, 3), ('T', 10, 0), ('T', 10, 1), ('R', 8, 3, 'S'), ('C', 10, 0, 'S'), ('C', 10, 1, 'S'), ('W', 12, 0, 0, 'V'), ('W', 12, 0, 1, 'V'), ('W', 12, 1, 0, 'S'), ('W', 12, 1, 1, 'S'), ('M', 9, 0), ('R', 9, 0, 'V'), ('M', 9, 1), ('R', 9, 1, 'V'), ('Q', 10), ('M', 9, 2), ('R', 9, 2, 'V'), ('M', 9, 3), ('Z', 0, 0), ('E', 0, 0), ('T', 11, 0), ('T', 11, 1), ('R', 9, 3, 'V'), ('C', 11, 0, 'S'), ('C', 11, 1, 'S'), ('W', 13, 0, 0, 'V'), ('W', 13, 0, 1, 'S'), ('W', 13, 1, 0, 'S'), ('W', 13, 1, 1, 'S'), ('M', 10, 0), ('R', 10, 0, 'V'), ('M', 10, 1), ('R', 10, 1, 'V'), ('Q', 11), ('M', 10, 2), ('R', 10, 2, 'V'), ('M', 10, 3), ('Z', 0, 1), ('E', 0, 1), ('T', 12, 0), ('T', 12, 1), ('R', 10, 3, 'V'), ('K', 0, 0, 'V'), ('ST', 0, 0), ('C', 12, 0, 'S'), ('C', 12, 1, 'S'), ('W', 14, 0, 0, 'V'), ('W', 14, 0, 1, 'V'), ('W', 14, 1, 0, 'V'), ('W', 14, 1, 1, 'S'), ('M', 11, 0), ('R', 11, 0, 'V'), ('M', 11, 1), ('R', 11, 1, 'V'), ('Q', 12), ('M', 11, 2), ('R', 11, 2, 'V'), ('M', 11, 3), ('Z', 0, 2), ('E', 0, 2), ('T', 13, 0), ('T', 13, 1), ('R', 11, 3, 'V'), ('K', 0, 1, 'V'), ('ST', 0, 1), ('C', 13, 0, 'S'), ('C', 13, 1, 'S'), ('W', 15, 0, 0, 'V'), ('W', 15, 0, 1, 'S'), ('W', 15, 1, 0, 'S'), ('W', 15, 1, 1, 'S'), ('M', 12, 0), ('R', 12, 0, 'V'), ('M', 12, 1), ('R', 12, 1, 'V'), ('Q', 13), ('M', 12, 2), ('R', 12, 2, 'V'), ('M', 12, 3), ('Z', 0, 3), ('E', 0, 3), ('T', 14, 0), ('T', 14, 1), ('R', 12, 3, 'V'), ('K', 0, 2, 'V'), ('ST', 0, 2), ('C', 14, 0, 'S'), ('C', 14, 1, 'S'), ('M', 13, 0), ('R', 13, 0, 'V'), ('M', 13, 1), ('R', 13, 1, 'V'), ('Q', 14), ('M', 13, 2), ('R', 13, 2, 'V'), ('M', 13, 3), ('T', 15, 0), ('T', 15, 1), ('R', 13, 3, 'V'), ('K', 0, 3, 'V'), ('ST', 0, 3), ('C', 15, 0, 'S'), ('C', 15, 1, 'S'), ('M', 14, 0), ('R', 14, 0, 'V'), ('M', 14, 1), ('R', 14, 1, 'V'), ('Q', 15), ('M', 14, 2), ('R', 14, 2, 'V'), ('M', 14, 3), ('R', 14, 3, 'V'), ('M', 15, 0), ('R', 15, 0, 'V'), ('M', 15, 1), ('R', 15, 1, 'V'), ('AQ', 1, 0), ('M', 15, 2), ('R', 15, 2, 'V'), ('AQ', 1, 1), ('M', 15, 3), ('Z', 1, 0), ('R', 15, 3, 'V'), ('AQ', 1, 2), ('Z', 1, 1), ('E', 1, 0), ('AQ', 1, 3), ('K', 1, 0, 'V'), ('ST', 1, 0), ('E', 1, 1), ('K', 1, 1, 'V'), ('ST', 1, 1), ('Z', 1, 2), ('E', 1, 2), ('K', 1, 2, 'V'), ('ST', 1, 2), ('Z', 1, 3), ('E', 1, 3, 0, 2), ('E', 1, 3, 2, 4), ('K', 1, 3, 'V', 0, 2), ('ST', 1, 3, 0, 2), ('K', 1, 3, 'V', 2, 4), ('ST', 1, 3, 2, 4)]
+    return [('L', 'x0', 256), ('L', 'xs0', 64), ('L', 'x1', 256), ('L', 'w00', 512), ('L', 'x2', 256), ('L', 'w10', 512), ('L', 'x3', 256), ('L', 'w01', 512), ('L', 'w11', 512), ('L', 'x4', 256), ('L', 'x5', 256), ('L', 'xs1', 64), ('L', 'x6', 256), ('L', 'x7', 256), ('L', 'x8', 256), ('L', 'x9', 256), ('L', 'q', 600), ('L', 'mask', 1024), ('L', 'x10', 256), ('L', 'x11', 256), ('L', 'x12', 256), ('L', 'x13', 256), ('L', 'x14', 256), ('L', 'x15', 256), ('W', 0, 0, 1, 'V'), ('W', 0, 1, 1, 'V'), ('W', 0, 1, 0, 'V'), ('W', 0, 0, 0, 'S'), ('W', 1, 1, 0, 'V'), ('W', 1, 0, 0, 'S'), ('W', 1, 1, 1, 'S'), ('W', 1, 0, 1, 'S'), ('T', 0, 1), ('T', 1, 0), ('WI', 0, 0, 1, 'V'), ('W', 2, 1, 0, 'S'), ('WI', 0, 0, 0, 'V'), ('WQ', 0, 0, 1), ('WI', 1, 0, 0, 'V'), ('WI', 1, 0, 1, 'V'), ('C', 0, 1, 'S'), ('C', 1, 0, 'S'), ('W', 2, 1, 1, 'S'), ('T', 0, 0), ('W', 2, 0, 1, 'V'), ('T', 1, 1), ('WQ', 1, 0, 0), ('WQ', 1, 0, 1), ('W', 3, 1, 1, 'V'), ('C', 0, 0, 'S'), ('T', 2, 1), ('Q', 0), ('M', 0, 1), ('W', 3, 1, 0, 'S'), ('W', 3, 0, 1, 'V'), ('WQ', 0, 0, 0), ('WI', 0, 1, 0, 'V'), ('W', 2, 0, 0, 'S'), ('C', 1, 1, 'S'), ('Q', 1), ('WI', 1, 1, 0, 'V'), ('T', 3, 1), ('M', 0, 0), ('M', 1, 1), ('C', 2, 1, 'S'), ('W', 3, 0, 0, 'S'), ('WI', 0, 1, 1, 'V'), ('T', 3, 0), ('WQ', 0, 1, 0), ('WQ', 1, 1, 0), ('C', 3, 1, 'S'), ('T', 2, 0), ('M', 1, 0), ('M', 0, 2), ('WI', 1, 1, 1, 'S'), ('M', 1, 2), ('WQ', 0, 1, 1), ('WQ', 1, 1, 1), ('R', 0, 1, 'S'), ('C', 2, 0, 'S'), ('R', 1, 1, 'V'), ('Q', 2), ('W', 4, 1, 0, 'V'), ('R', 0, 0, 'S'), ('M', 0, 3), ('M', 2, 0), ('R', 1, 0, 'V'), ('W', 4, 0, 1, 'V'), ('M', 2, 1), ('C', 3, 0, 'S'), ('R', 0, 2, 'S'), ('R', 2, 0, 'V'), ('M', 2, 3), ('W', 4, 1, 1, 'S'), ('R', 1, 2, 'V'), ('W', 4, 0, 0, 'S'), ('R', 2, 1, 'V'), ('R', 0, 3, 'S'), ('W', 5, 0, 1, 'S'), ('M', 1, 3), ('W', 5, 0, 0, 'S'), ('Q', 3), ('R', 1, 3, 'V'), ('W', 5, 1, 0, 'S'), ('M', 2, 2), ('R', 2, 2, 'V'), ('W', 5, 1, 1, 'V'), ('T', 4, 0), ('T', 4, 1), ('R', 2, 3, 'V'), ('C', 4, 0, 'S'), ('C', 4, 1, 'S'), ('W', 6, 0, 0, 'S'), ('W', 6, 0, 1, 'S'), ('W', 6, 1, 0, 'S'), ('W', 6, 1, 1, 'S'), ('M', 3, 0), ('R', 3, 0, 'V'), ('M', 3, 1), ('R', 3, 1, 'V'), ('Q', 4), ('M', 3, 2), ('R', 3, 2, 'V'), ('M', 3, 3), ('T', 5, 0), ('T', 5, 1), ('R', 3, 3, 'V'), ('C', 5, 0, 'S'), ('C', 5, 1, 'S'), ('W', 7, 0, 0, 'V'), ('W', 7, 0, 1, 'S'), ('W', 7, 1, 0, 'S'), ('W', 7, 1, 1, 'S'), ('M', 4, 0), ('R', 4, 0, 'V'), ('M', 4, 1), ('R', 4, 1, 'V'), ('Q', 5), ('M', 4, 2), ('R', 4, 2, 'V'), ('M', 4, 3), ('T', 6, 0), ('T', 6, 1), ('R', 4, 3, 'V'), ('C', 6, 0, 'S'), ('C', 6, 1, 'S'), ('W', 8, 0, 0, 'V'), ('W', 8, 0, 1, 'S'), ('W', 8, 1, 0, 'S'), ('W', 8, 1, 1, 'S'), ('M', 5, 0), ('R', 5, 0, 'V'), ('M', 5, 1), ('R', 5, 1, 'V'), ('Q', 6), ('M', 5, 2), ('R', 5, 2, 'V'), ('M', 5, 3), ('T', 7, 0), ('T', 7, 1), ('R', 5, 3, 'V'), ('C', 7, 0, 'S'), ('C', 7, 1, 'S'), ('W', 9, 0, 0, 'V'), ('W', 9, 0, 1, 'S'), ('W', 9, 1, 0, 'S'), ('W', 9, 1, 1, 'S'), ('M', 6, 0), ('R', 6, 0, 'V'), ('M', 6, 1), ('R', 6, 1, 'V'), ('Q', 7), ('M', 6, 2), ('R', 6, 2, 'V'), ('M', 6, 3), ('T', 8, 0), ('T', 8, 1), ('R', 6, 3, 'V'), ('C', 8, 0, 'S'), ('C', 8, 1, 'S'), ('W', 10, 0, 0, 'V'), ('W', 10, 0, 1, 'S'), ('W', 10, 1, 0, 'S'), ('W', 10, 1, 1, 'S'), ('M', 7, 0), ('R', 7, 0, 'V'), ('M', 7, 1), ('R', 7, 1, 'V'), ('AQ', 0, 0), ('Q', 8), ('AQ', 0, 1), ('M', 7, 2), ('R', 7, 2, 'V'), ('M', 7, 3), ('T', 9, 0), ('T', 9, 1), ('R', 7, 3, 'V'), ('AQ', 0, 2), ('C', 9, 0, 'S'), ('C', 9, 1, 'S'), ('Q', 9), ('AQ', 0, 3), ('W', 11, 0, 0, 'V'), ('W', 11, 0, 1, 'V'), ('W', 11, 1, 0, 'V'), ('W', 11, 1, 1, 'V'), ('M', 8, 0), ('R', 8, 0, 'S'), ('M', 8, 1), ('R', 8, 1, 'S'), ('M', 8, 2), ('R', 8, 2, 'S'), ('M', 8, 3), ('T', 10, 0), ('T', 10, 1), ('R', 8, 3, 'S'), ('C', 10, 0, 'S'), ('C', 10, 1, 'S'), ('W', 12, 0, 0, 'V'), ('W', 12, 0, 1, 'S'), ('W', 12, 1, 0, 'S'), ('W', 12, 1, 1, 'S'), ('M', 9, 0), ('R', 9, 0, 'V'), ('M', 9, 1), ('R', 9, 1, 'V'), ('Q', 10), ('M', 9, 2), ('R', 9, 2, 'V'), ('M', 9, 3), ('Z', 0, 0), ('E', 0, 0), ('T', 11, 0), ('T', 11, 1), ('R', 9, 3, 'V'), ('C', 11, 0, 'S'), ('C', 11, 1, 'S'), ('W', 13, 0, 0, 'V'), ('W', 13, 0, 1, 'S'), ('W', 13, 1, 0, 'S'), ('W', 13, 1, 1, 'S'), ('M', 10, 0), ('R', 10, 0, 'V'), ('M', 10, 1), ('R', 10, 1, 'V'), ('Q', 11), ('M', 10, 2), ('R', 10, 2, 'V'), ('M', 10, 3), ('Z', 0, 1), ('E', 0, 1), ('T', 12, 0), ('T', 12, 1), ('R', 10, 3, 'V'), ('K', 0, 0, 'V'), ('ST', 0, 0), ('C', 12, 0, 'S'), ('C', 12, 1, 'S'), ('W', 14, 0, 0, 'V'), ('W', 14, 0, 1, 'S'), ('W', 14, 1, 0, 'S'), ('W', 14, 1, 1, 'S'), ('M', 11, 0), ('R', 11, 0, 'V'), ('M', 11, 1), ('R', 11, 1, 'V'), ('Q', 12), ('M', 11, 2), ('R', 11, 2, 'V'), ('M', 11, 3), ('Z', 0, 2), ('E', 0, 2), ('T', 13, 0), ('T', 13, 1), ('R', 11, 3, 'V'), ('K', 0, 1, 'V'), ('ST', 0, 1), ('C', 13, 0, 'S'), ('C', 13, 1, 'S'), ('W', 15, 0, 0, 'V'), ('W', 15, 0, 1, 'S'), ('W', 15, 1, 0, 'S'), ('W', 15, 1, 1, 'S'), ('M', 12, 0), ('R', 12, 0, 'V'), ('M', 12, 1), ('R', 12, 1, 'V'), ('Q', 13), ('M', 12, 2), ('R', 12, 2, 'V'), ('M', 12, 3), ('Z', 0, 3), ('E', 0, 3), ('T', 14, 0), ('T', 14, 1), ('R', 12, 3, 'V'), ('K', 0, 2, 'V'), ('ST', 0, 2), ('C', 14, 0, 'S'), ('C', 14, 1, 'S'), ('M', 13, 0), ('R', 13, 0, 'V'), ('M', 13, 1), ('R', 13, 1, 'V'), ('Q', 14), ('M', 13, 2), ('R', 13, 2, 'V'), ('M', 13, 3), ('T', 15, 0), ('T', 15, 1), ('R', 13, 3, 'V'), ('K', 0, 3, 'V'), ('ST', 0, 3), ('C', 15, 0, 'S'), ('C', 15, 1, 'S'), ('M', 14, 0), ('R', 14, 0, 'V'), ('M', 14, 1), ('R', 14, 1, 'V'), ('Q', 15), ('M', 14, 2), ('R', 14, 2, 'V'), ('M', 14, 3), ('R', 14, 3, 'V'), ('M', 15, 0), ('R', 15, 0, 'V'), ('M', 15, 1), ('R', 15, 1, 'V'), ('AQ', 1, 0), ('M', 15, 2), ('R', 15, 2, 'V'), ('AQ', 1, 1), ('AQ', 1, 2), ('M', 15, 3), ('Z', 1, 0), ('R', 15, 3, 'V'), ('Z', 1, 1), ('AQ', 1, 3), ('E', 1, 0), ('K', 1, 0, 'V'), ('ST', 1, 0), ('E', 1, 1), ('K', 1, 1, 'V'), ('ST', 1, 1),
+ ('Z', 1, 2, 0, 2, 0, 1), ('Z', 1, 2, 2, 4, 0, 1), ('Z', 1, 3, 0, 2, 0, 1), ('Z', 1, 3, 2, 4, 0, 1),
+ ('Z', 1, 2, 0, 2, 1), ('E', 1, 2, 0, 2), ('K', 1, 2, 'V', 0, 2), ('ST', 1, 2, 0, 2),
+ ('Z', 1, 2, 2, 4, 1), ('E', 1, 2, 2, 4), ('K', 1, 2, 'V', 2, 4), ('ST', 1, 2, 2, 4),
+ ('Z', 1, 3, 0, 2, 1), ('E', 1, 3, 0, 2), ('K', 1, 3, 'V', 0, 2), ('ST', 1, 3, 0, 2),
+ ('Z', 1, 3, 2, 4, 1), ('E', 1, 3, 2, 4), ('K', 1, 3, 'V', 2, 4), ('ST', 1, 3, 2, 4)]
 
 
 def tile_masked_block_scores_d4_kernel(tc, x_bytes, x_scale, w, query_words, query_scales, mask, out):
@@ -27,7 +32,7 @@ def tile_masked_block_scores_d4_kernel(tc, x_bytes, x_scale, w, query_words, que
     with ExitStack() as ctx:
         keep = ctx.enter_context(tc.tile_pool(name="keep", bufs=1))
         work = ctx.enter_context(tc.tile_pool(name="work", bufs=3))
-        tps = ctx.enter_context(tc.psum_pool(name="tps", bufs=1))
+        tps = ctx.enter_context(tc.psum_pool(name="tps", bufs=2))
         mps = ctx.enter_context(tc.psum_pool(name="mps", bufs=6))
 
         ident = keep.tile([P, P], F32, name="ident")
@@ -101,7 +106,7 @@ def tile_masked_block_scores_d4_kernel(tc, x_bytes, x_scale, w, query_words, que
                     )
 
         def turn(s, g):
-            bank = tps.tile([P, 2, 2, P], F32, name="turned%d" % g)
+            bank = tps.tile([P, 2, 2, P], F32, name="turned")
             live["turned", s, g] = bank
             for c in range(2):
                 words = live["wide", s, g, c][:].bitcast(F32)
@@ -182,7 +187,7 @@ def tile_masked_block_scores_d4_kernel(tc, x_bytes, x_scale, w, query_words, que
                 nc.vector.scalar_tensor_tensor(out=total, in0=bank, scalar=0.0, in1=total, op0=ALU.max, op1=ALU.add)
 
         def group_w(g, G, tp, eng):
-            grouped = work.tile([P, 2, P, 4], BF16, name="w_grouped", align_bytes=64, bufs=4)
+            grouped = work.tile([P, 2, P, 4], BF16, name="w_grouped", align_bytes=64, bufs=8)
             live["wg", g, G, tp] = grouped
             src = w_raw[g, G][:].rearrange("p j (m t) -> p t m j", t=4)[:, 2 * tp : 2 * tp + 2]
             if eng == "S":
@@ -205,32 +210,33 @@ def tile_masked_block_scores_d4_kernel(tc, x_bytes, x_scale, w, query_words, que
             live["aq", h, b] = (codes, scales)
             nc.vector.quantize_mx(out=codes[:].bitcast(FP8X4), scales=scales[:], in_=live["ag", h, b][:].rearrange("p n t -> p (n t)"))
 
-        def scores(h, b):
+        def scores(h, b, lo=0, hi=4, first=0, last=None):
             c, qh = b // 2, b % 2
-            bank = mps.tile([P, 4, P], F32, name="bank")
-            live["z", h, b] = bank
-            for qq in range(4):
+            if first == 0:
+                live["z", h, b, lo] = mps.tile([P, hi - lo, P], F32, name="bank")
+            bank = live["z", h, b, lo]
+            passes = [(qq, g) for qq in range(lo, hi) for g in range(2)]
+            for qq, g in passes[first:last]:
                 qt = 4 * qh + qq
-                for g in range(2):
-                    codes, scales = live["aq", h, 2 * c + g]
-                    nc.tensor.matmul_mx(
-                        out=bank[:, qq, :],
-                        lhsT=q_words[:, g, 2 * P * qt : 2 * P * (qt + 1)].bitcast(FP4X4),
-                        lhsT_scale=q_scales[:, g, P * qt : P * (qt + 1)],
-                        rhs=codes[:].bitcast(FP8X4),
-                        rhs_scale=scales[:],
-                        start=(g == 0),
-                        stop=(g == 1),
-                    )
+                codes, scales = live["aq", h, 2 * c + g]
+                nc.tensor.matmul_mx(
+                    out=bank[:, qq - lo, :],
+                    lhsT=q_words[:, g, 2 * P * qt : 2 * P * (qt + 1)].bitcast(FP4X4),
+                    lhsT_scale=q_scales[:, g, P * qt : P * (qt + 1)],
+                    rhs=codes[:].bitcast(FP8X4),
+                    rhs_scale=scales[:],
+                    start=(g == 0),
+                    stop=(g == 1),
+                )
 
         def window(h, b, lo, hi):
             c, qh = b // 2, b % 2
             return slice(4 * qh + lo, 4 * qh + hi), slice(256 * h + P * c, 256 * h + P * (c + 1))
 
         def expo(h, b, lo=0, hi=4):
-            e = work.tile([P, hi - lo, P], F32, name="expo", bufs=4)
+            e = work.tile([P, hi - lo, P], F32, name="expo", bufs=8)
             live["e", h, b, lo] = e
-            nc.scalar.activation(out=e[:], in_=live["z", h, b][:, lo:hi, :], func=ACT.Exp, scale=1.0 / C)
+            nc.scalar.activation(out=e[:], in_=live["z", h, b, lo][:], func=ACT.Exp, scale=1.0 / C)
 
         def masked(h, b, eng, lo=0, hi=4):
             e = live["e", h, b, lo]

from contextlib import ExitStack

import concourse.mybir as mybir
from concourse.masks import make_identity

F32 = mybir.dt.float32
BF16 = mybir.dt.bfloat16
U32 = mybir.dt.uint32
I32 = mybir.dt.int32
U8 = mybir.dt.uint8
FP8 = mybir.dt.float8_e4m3fn
FP8X4 = mybir.dt.float8_e4m3fn_x4
FP4X4 = mybir.dt.float4_e2m1fn_x4
ALU = mybir.AluOpType
ACT = mybir.ActivationFunctionType

T, K, N, M, C = 4096, 1024, 1024, 1024, 8
P = 128
FLOPS = 2 * T * K * N + 2 * M * N * (T // C)

def build_order():
    return [('L', 'x0', 256), ('L', 'xs0', 64), ('L', 'x1', 256), ('L', 'w00', 512), ('L', 'x2', 256), ('L', 'w10', 512), ('L', 'x3', 256), ('L', 'w01', 512), ('L', 'w11', 512), ('L', 'x4', 256), ('L', 'x5', 256), ('L', 'xs1', 64), ('L', 'x6', 256), ('L', 'x7', 256), ('L', 'x8', 256), ('L', 'x9', 256), ('L', 'q', 600), ('L', 'mask', 1024), ('L', 'x10', 256), ('L', 'x11', 256), ('L', 'x12', 256), ('L', 'x13', 256), ('L', 'x14', 256), ('L', 'x15', 256), ('W', 0, 0, 1, 'V'), ('W', 0, 1, 1, 'V'), ('W', 0, 1, 0, 'V'), ('W', 0, 0, 0, 'S'), ('W', 1, 1, 0, 'V'), ('W', 1, 0, 0, 'S'), ('W', 1, 1, 1, 'S'), ('W', 1, 0, 1, 'S'), ('T', 0, 1), ('T', 1, 0), ('WI', 0, 0, 1, 'V'), ('W', 2, 1, 0, 'S'), ('WI', 0, 0, 0, 'V'), ('WQ', 0, 0, 1), ('WI', 1, 0, 0, 'V'), ('WI', 1, 0, 1, 'V'), ('C', 0, 1, 'S'), ('C', 1, 0, 'S'), ('W', 2, 1, 1, 'S'), ('T', 0, 0), ('W', 2, 0, 1, 'V'), ('T', 1, 1), ('WQ', 1, 0, 0), ('WQ', 1, 0, 1), ('W', 3, 1, 1, 'V'), ('C', 0, 0, 'S'), ('T', 2, 1), ('Q', 0), ('M', 0, 1), ('W', 3, 1, 0, 'S'), ('W', 3, 0, 1, 'V'), ('WQ', 0, 0, 0), ('WI', 0, 1, 0, 'V'), ('W', 2, 0, 0, 'S'), ('C', 1, 1, 'S'), ('Q', 1), ('WI', 1, 1, 0, 'V'), ('T', 3, 1), ('M', 0, 0), ('M', 1, 1), ('C', 2, 1, 'S'), ('W', 3, 0, 0, 'S'), ('WI', 0, 1, 1, 'V'), ('T', 3, 0), ('WQ', 0, 1, 0), ('WQ', 1, 1, 0), ('C', 3, 1, 'S'), ('T', 2, 0), ('M', 1, 0), ('M', 0, 2), ('WI', 1, 1, 1, 'S'), ('M', 1, 2), ('WQ', 0, 1, 1), ('WQ', 1, 1, 1), ('R', 0, 1, 'S'), ('C', 2, 0, 'S'), ('R', 1, 1, 'V'), ('Q', 2), ('W', 4, 1, 0, 'V'), ('R', 0, 0, 'S'), ('M', 0, 3), ('M', 2, 0), ('R', 1, 0, 'V'), ('W', 4, 0, 1, 'V'), ('M', 2, 1), ('C', 3, 0, 'S'), ('R', 0, 2, 'S'), ('R', 2, 0, 'V'), ('M', 2, 3), ('W', 4, 1, 1, 'S'), ('R', 1, 2, 'V'), ('W', 4, 0, 0, 'S'), ('R', 2, 1, 'V'), ('R', 0, 3, 'S'), ('W', 5, 0, 1, 'S'), ('M', 1, 3), ('W', 5, 0, 0, 'S'), ('Q', 3), ('R', 1, 3, 'V'), ('W', 5, 1, 0, 'S'), ('M', 2, 2), ('R', 2, 2, 'V'), ('W', 5, 1, 1, 'V'), ('T', 4, 0), ('T', 4, 1), ('R', 2, 3, 'V'), ('C', 4, 0, 'S'), ('C', 4, 1, 'S'), ('W', 6, 0, 0, 'S'), ('W', 6, 0, 1, 'S'), ('W', 6, 1, 0, 'S'), ('W', 6, 1, 1, 'S'), ('M', 3, 0), ('R', 3, 0, 'V'), ('M', 3, 1), ('R', 3, 1, 'V'), ('Q', 4), ('M', 3, 2), ('R', 3, 2, 'V'), ('M', 3, 3), ('T', 5, 0), ('T', 5, 1), ('R', 3, 3, 'V'), ('C', 5, 0, 'S'), ('C', 5, 1, 'S'), ('W', 7, 0, 0, 'V'), ('W', 7, 0, 1, 'S'), ('W', 7, 1, 0, 'S'), ('W', 7, 1, 1, 'S'), ('M', 4, 0), ('R', 4, 0, 'V'), ('M', 4, 1), ('R', 4, 1, 'V'), ('Q', 5), ('M', 4, 2), ('R', 4, 2, 'V'), ('M', 4, 3), ('T', 6, 0), ('T', 6, 1), ('R', 4, 3, 'V'), ('C', 6, 0, 'S'), ('C', 6, 1, 'S'), ('W', 8, 0, 0, 'V'), ('W', 8, 0, 1, 'S'), ('W', 8, 1, 0, 'S'), ('W', 8, 1, 1, 'S'), ('M', 5, 0), ('R', 5, 0, 'V'), ('M', 5, 1), ('R', 5, 1, 'V'), ('Q', 6), ('M', 5, 2), ('R', 5, 2, 'V'), ('M', 5, 3), ('T', 7, 0), ('T', 7, 1), ('R', 5, 3, 'V'), ('C', 7, 0, 'S'), ('C', 7, 1, 'S'), ('W', 9, 0, 0, 'V'), ('W', 9, 0, 1, 'S'), ('W', 9, 1, 0, 'S'), ('W', 9, 1, 1, 'S'), ('M', 6, 0), ('R', 6, 0, 'V'), ('M', 6, 1), ('R', 6, 1, 'V'), ('Q', 7), ('M', 6, 2), ('R', 6, 2, 'V'), ('M', 6, 3), ('T', 8, 0), ('T', 8, 1), ('R', 6, 3, 'V'), ('C', 8, 0, 'S'), ('C', 8, 1, 'S'), ('W', 10, 0, 0, 'V'), ('W', 10, 0, 1, 'S'), ('W', 10, 1, 0, 'S'), ('W', 10, 1, 1, 'S'), ('M', 7, 0), ('R', 7, 0, 'V'), ('M', 7, 1), ('R', 7, 1, 'V'), ('AQ', 0, 0), ('Q', 8), ('AQ', 0, 1), ('M', 7, 2), ('R', 7, 2, 'V'), ('M', 7, 3), ('T', 9, 0), ('T', 9, 1), ('R', 7, 3, 'V'), ('AQ', 0, 2), ('C', 9, 0, 'S'), ('C', 9, 1, 'S'), ('Q', 9), ('AQ', 0, 3), ('W', 11, 0, 0, 'V'), ('W', 11, 0, 1, 'V'), ('W', 11, 1, 0, 'V'), ('W', 11, 1, 1, 'V'), ('M', 8, 0), ('R', 8, 0, 'S'), ('M', 8, 1), ('R', 8, 1, 'S'), ('M', 8, 2), ('R', 8, 2, 'S'), ('M', 8, 3), ('T', 10, 0), ('T', 10, 1), ('R', 8, 3, 'S'), ('C', 10, 0, 'S'), ('C', 10, 1, 'S'), ('W', 12, 0, 0, 'V'), ('W', 12, 0, 1, 'S'), ('W', 12, 1, 0, 'S'), ('W', 12, 1, 1, 'S'), ('M', 9, 0), ('R', 9, 0, 'V'), ('M', 9, 1), ('R', 9, 1, 'V'), ('Q', 10), ('M', 9, 2), ('R', 9, 2, 'V'), ('M', 9, 3), ('Z', 0, 0), ('E', 0, 0), ('T', 11, 0), ('T', 11, 1), ('R', 9, 3, 'V'), ('C', 11, 0, 'S'), ('C', 11, 1, 'S'), ('W', 13, 0, 0, 'V'), ('W', 13, 0, 1, 'S'), ('W', 13, 1, 0, 'S'), ('W', 13, 1, 1, 'S'), ('M', 10, 0), ('R', 10, 0, 'V'), ('M', 10, 1), ('R', 10, 1, 'V'), ('Q', 11), ('M', 10, 2), ('R', 10, 2, 'V'), ('M', 10, 3), ('Z', 0, 1), ('E', 0, 1), ('T', 12, 0), ('T', 12, 1), ('R', 10, 3, 'V'), ('K', 0, 0, 'V'), ('ST', 0, 0), ('C', 12, 0, 'S'), ('C', 12, 1, 'S'), ('W', 14, 0, 0, 'V'), ('W', 14, 0, 1, 'S'), ('W', 14, 1, 0, 'S'), ('W', 14, 1, 1, 'S'), ('M', 11, 0), ('R', 11, 0, 'V'), ('M', 11, 1), ('R', 11, 1, 'V'), ('Q', 12), ('M', 11, 2), ('R', 11, 2, 'V'), ('M', 11, 3), ('Z', 0, 2), ('E', 0, 2), ('T', 13, 0), ('T', 13, 1), ('R', 11, 3, 'V'), ('K', 0, 1, 'V'), ('ST', 0, 1), ('C', 13, 0, 'S'), ('C', 13, 1, 'S'), ('W', 15, 0, 0, 'V'), ('W', 15, 0, 1, 'S'), ('W', 15, 1, 0, 'S'), ('W', 15, 1, 1, 'S'), ('M', 12, 0), ('R', 12, 0, 'V'), ('M', 12, 1), ('R', 12, 1, 'V'), ('Q', 13), ('M', 12, 2), ('R', 12, 2, 'V'), ('M', 12, 3), ('Z', 0, 3), ('E', 0, 3), ('T', 14, 0), ('T', 14, 1), ('R', 12, 3, 'V'), ('K', 0, 2, 'V'), ('ST', 0, 2), ('C', 14, 0, 'S'), ('C', 14, 1, 'S'), ('M', 13, 0), ('R', 13, 0, 'V'), ('M', 13, 1), ('R', 13, 1, 'V'), ('Q', 14), ('M', 13, 2), ('R', 13, 2, 'V'), ('M', 13, 3), ('T', 15, 0), ('T', 15, 1), ('R', 13, 3, 'V'), ('K', 0, 3, 'V'), ('ST', 0, 3), ('C', 15, 0, 'S'), ('C', 15, 1, 'S'), ('M', 14, 0), ('R', 14, 0, 'V'), ('M', 14, 1), ('R', 14, 1, 'V'), ('Q', 15), ('M', 14, 2), ('R', 14, 2, 'V'), ('M', 14, 3), ('R', 14, 3, 'V'), ('M', 15, 0), ('R', 15, 0, 'V'), ('M', 15, 1), ('R', 15, 1, 'V'), ('AQ', 1, 0), ('M', 15, 2), ('R', 15, 2, 'V'), ('AQ', 1, 1), ('AQ', 1, 2), ('M', 15, 3), ('Z', 1, 0), ('R', 15, 3, 'V'), ('Z', 1, 1), ('AQ', 1, 3), ('E', 1, 0), ('K', 1, 0, 'V'), ('ST', 1, 0), ('E', 1, 1), ('K', 1, 1, 'V'), ('ST', 1, 1),
 ('Z', 1, 2, 0, 2, 0, 1), ('Z', 1, 2, 2, 4, 0, 1), ('Z', 1, 3, 0, 2, 0, 1), ('Z', 1, 3, 2, 4, 0, 1),
 ('Z', 1, 2, 0, 2, 1), ('E', 1, 2, 0, 2), ('K', 1, 2, 'V', 0, 2), ('ST', 1, 2, 0, 2),
 ('Z', 1, 2, 2, 4, 1), ('E', 1, 2, 2, 4), ('K', 1, 2, 'V', 2, 4), ('ST', 1, 2, 2, 4),
 ('Z', 1, 3, 0, 2, 1), ('E', 1, 3, 0, 2), ('K', 1, 3, 'V', 0, 2), ('ST', 1, 3, 0, 2),
 ('Z', 1, 3, 2, 4, 1), ('E', 1, 3, 2, 4), ('K', 1, 3, 'V', 2, 4), ('ST', 1, 3, 2, 4)]


def tile_masked_block_scores_d4_kernel(tc, x_bytes, x_scale, w, query_words, query_scales, mask, out):
    nc = tc.nc
    with ExitStack() as ctx:
        keep = ctx.enter_context(tc.tile_pool(name="keep", bufs=1))
        work = ctx.enter_context(tc.tile_pool(name="work", bufs=3))
        tps = ctx.enter_context(tc.psum_pool(name="tps", bufs=2))
        mps = ctx.enter_context(tc.psum_pool(name="mps", bufs=6))

        ident = keep.tile([P, P], F32, name="ident")
        make_identity(nc, ident[:])
        q_scales = keep.tile([P, 2, M], U8, name="q_scales", align_bytes=64)
        nc.gpsimd.memset(q_scales[:].rearrange("p g n -> p (g n)").bitcast(I32), 0)
        q_words = keep.tile([P, 2, 2 * M], U8, name="q_words", align_bytes=64)
        mask_sb = keep.tile([P, 8, 512], BF16, name="mask_sb")
        xs = [keep.tile([P, 2, 64], F32, name="xs%d" % h) for h in range(2)]
        xb = [keep.tile([P, 2, K], U8, name="xbytes%d" % s) for s in range(16)]
        w_raw = {(g, G): keep.tile([P, 4, 512], BF16, name="w_raw%d%d" % (g, G)) for g in range(2) for G in range(2)}
        w_codes = {}
        w_scales = {}
        for g in range(2):
            for G in range(2):
                for tp in range(2):
                    w_codes[g, G, tp] = keep.tile([P, 256], U32, name="w_codes%d%d%d" % (g, G, tp), align_bytes=64)
                    w_scales[g, G, tp] = keep.tile([P, 256], U8, name="w_scales%d%d%d" % (g, G, tp), align_bytes=64)
        acc2 = {(h, G): keep.tile([P, 4, 256], F32, name="acc%d%d" % (h, G)) for h in range(2) for G in range(2)}
        warm = keep.tile([P, 2], F32, name="warm")

        x_view = x_bytes.rearrange("(h c p j) k -> h j p c k", h=2, c=2, p=P)
        xs_view = x_scale.rearrange("(h c p j) b -> h p c (j b)", h=2, c=2, p=P)
        out_view = out.rearrange("(t p) b -> p t b", p=P)
        live = {}

        ctx.enter_context(tc.manual_schedule())
        nc.vector.memset(warm[:, 0:1], 0.0)
        nc.scalar.activation(out=warm[:, 1:2], in_=warm[:, 0:1], func=ACT.Exp)

        def load(name):
            if name.startswith("xs"):
                h = int(name[2:])
                nc.sync.dma_start(out=xs[h][:], in_=xs_view[h])
            elif name.startswith("x"):
                s = int(name[1:])
                nc.sync.dma_start(out=xb[s][:], in_=x_view[s // 8, s % 8])
            elif name.startswith("w"):
                g, G = int(name[1]), int(name[2])
                rows = w[512 * g : 512 * (g + 1), 512 * G : 512 * (G + 1)]
                nc.sync.dma_start(out=w_raw[g, G][:], in_=rows.rearrange("(p j) n -> p j n", j=4))
            elif name == "q":
                for quad in range(4):
                    nc.sync.dma_start(
                        out=q_scales[32 * quad : 32 * quad + 4, :, :].bitcast(I32),
                        in_=query_scales[:, 4 * quad : 4 * quad + 4, :].rearrange("g r n -> r g n").bitcast(I32),
                    )
                nc.sync.dma_start(out=q_words[:].bitcast(I32), in_=query_words.rearrange("g p n -> p g n").bitcast(I32))
            else:
                nc.sync.dma_start(out=mask_sb[:], in_=mask.rearrange("(t p) b -> p t b", p=P))

        def wide_tile(s, g, c):
            live["wide", s, g, c] = work.tile([P, 512], BF16, name="wide%d%d" % (g, c), bufs=6)
            return live["wide", s, g, c]

        def widen(s, g, c, eng):
            dst = wide_tile(s, g, c)
            live["split", s, g, c] = eng == "V"
            halves = dst[:].rearrange("p (u w e) -> p w u e", u=2, e=2)
            for q in range(4):
                blk = 4 * g + q
                src = xb[s][:, c, P * blk : P * (blk + 1)].bitcast(FP8)
                scale = xs[s // 8][:, c, 8 * (s % 8) + blk : 8 * (s % 8) + blk + 1]
                if eng == "S":
                    nc.scalar.activation(out=dst[:, P * q : P * (q + 1)], in_=src, func=ACT.Copy, scale=scale)
                else:
                    nc.vector.tensor_scalar(
                        out=halves[:, 32 * q : 32 * (q + 1)],
                        in0=src.rearrange("p (w u e) -> p w u e", u=2, e=2),
                        scalar1=scale, scalar2=None, op0=ALU.mult,
                    )

        def turn(s, g):
            bank = tps.tile([P, 2, 2, P], F32, name="turned")
            live["turned", s, g] = bank
            for c in range(2):
                words = live["wide", s, g, c][:].bitcast(F32)
                for u in range(2):
                    src = words[:, P * u : P * (u + 1)] if live["split", s, g, c] else words[:, u : 2 * P : 2]
                    nc.tensor.transpose(bank[:, c, u, :], src, ident[:])

        def copy_out(s, g, eng):
            if ("grouped", s) not in live:
                live["grouped", s] = work.tile([P, 2, 1024], BF16, name="x_grouped", align_bytes=64)
            dst = live["grouped", s][:, g, :].bitcast(F32).rearrange("p (c r u) -> p c r u", c=2, u=2)
            src = live["turned", s, g][:].rearrange("p c u r -> p c r u")
            if eng == "S":
                nc.scalar.copy(out=dst, in_=src)
            else:
                nc.vector.tensor_copy(out=dst, in_=src)

        def quant_x(s):
            codes = work.tile([P, 512], U32, name="x_codes", align_bytes=64, bufs=4)
            scales = work.tile([P, 512], U8, name="x_scales", align_bytes=64, bufs=4)
            live["xq", s] = (codes, scales)
            nc.vector.quantize_mx(out=codes[:].bitcast(FP8X4), scales=scales[:], in_=live["grouped", s][:].rearrange("p g n -> p (g n)"))

        def features(s, b):
            G, tp = b // 2, b % 2
            bank = mps.tile([P, 2, 256], F32, name="bank")
            live["h", s, b] = bank
            codes, scales = live["xq", s]
            if s % 8 == 7:
                c, G = b // 2, b % 2
                quarters = bank[:].rearrange("p a (b n) -> p (a b) n", n=P)
                for t in range(4):
                    for g in range(2):
                        cols = slice(256 * g + P * c, 256 * g + P * (c + 1))
                        nc.tensor.matmul_mx(
                            out=quarters[:, t, :],
                            lhsT=w_codes[g, G, t // 2][:, P * (t % 2) : P * (t % 2 + 1)].bitcast(FP8X4),
                            lhsT_scale=w_scales[g, G, t // 2][:, P * (t % 2) : P * (t % 2 + 1)],
                            rhs=codes[:, cols].bitcast(FP8X4),
                            rhs_scale=scales[:, cols],
                            start=(g == 0),
                            stop=(g == 1),
                        )
                return
            for tt in range(2):
                for g in range(2):
                    nc.tensor.matmul_mx(
                        out=bank[:, tt, :],
                        lhsT=w_codes[g, G, tp][:, P * tt : P * (tt + 1)].bitcast(FP8X4),
                        lhsT_scale=w_scales[g, G, tp][:, P * tt : P * (tt + 1)],
                        rhs=codes[:, 256 * g : 256 * (g + 1)].bitcast(FP8X4),
                        rhs_scale=scales[:, 256 * g : 256 * (g + 1)],
                        start=(g == 0),
                        stop=(g == 1),
                    )

        def relu_sum(s, b, eng):
            if s % 8 == 7:
                c, G = b // 2, b % 2
                grouped = work.tile([P, P, 4], BF16, name="a_grouped", align_bytes=64, bufs=4)
                live["ag", s // 8, b] = grouped
                nc.vector.scalar_tensor_tensor(
                    out=grouped[:],
                    in0=live["h", s, b][:].rearrange("p a (b n) -> p n (a b)", n=P),
                    scalar=0.0,
                    in1=acc2[s // 8, G][:, :, P * c : P * (c + 1)].rearrange("p t n -> p n t"),
                    op0=ALU.max,
                    op1=ALU.add,
                )
                return
            bank = live["h", s, b][:].rearrange("p t n -> p (t n)")
            total = acc2[s // 8, b // 2][:, 2 * (b % 2) : 2 * (b % 2) + 2, :].rearrange("p t n -> p (t n)")
            if s % 8 == 0 and eng == "S":
                nc.scalar.activation(out=total, in_=bank, func=ACT.Relu)
            elif s % 8 == 0:
                nc.vector.tensor_scalar(out=total, in0=bank, scalar1=0.0, scalar2=None, op0=ALU.max)
            else:
                nc.vector.scalar_tensor_tensor(out=total, in0=bank, scalar=0.0, in1=total, op0=ALU.max, op1=ALU.add)

        def group_w(g, G, tp, eng):
            grouped = work.tile([P, 2, P, 4], BF16, name="w_grouped", align_bytes=64, bufs=8)
            live["wg", g, G, tp] = grouped
            src = w_raw[g, G][:].rearrange("p j (m t) -> p t m j", t=4)[:, 2 * tp : 2 * tp + 2]
            if eng == "S":
                nc.scalar.copy(out=grouped[:], in_=src)
            elif eng == "G":
                nc.gpsimd.tensor_scalar(out=grouped[:], in0=src, scalar1=1.0, scalar2=0.0, op0=ALU.mult, op1=ALU.add)
            else:
                nc.vector.tensor_copy(out=grouped[:], in_=src)

        def quant_w(g, G, tp):
            nc.vector.quantize_mx(
                out=w_codes[g, G, tp][:].bitcast(FP8X4),
                scales=w_scales[g, G, tp][:],
                in_=live["wg", g, G, tp][:].rearrange("p t m j -> p (t m j)"),
            )

        def quant_a(h, b):
            codes = work.tile([P, P], U32, name="a_codes", align_bytes=64, bufs=8)
            scales = work.tile([P, P], U8, name="a_scales", align_bytes=64, bufs=8)
            live["aq", h, b] = (codes, scales)
            nc.vector.quantize_mx(out=codes[:].bitcast(FP8X4), scales=scales[:], in_=live["ag", h, b][:].rearrange("p n t -> p (n t)"))

        def scores(h, b, lo=0, hi=4, first=0, last=None):
            c, qh = b // 2, b % 2
            if first == 0:
                live["z", h, b, lo] = mps.tile([P, hi - lo, P], F32, name="bank")
            bank = live["z", h, b, lo]
            passes = [(qq, g) for qq in range(lo, hi) for g in range(2)]
            for qq, g in passes[first:last]:
                qt = 4 * qh + qq
                codes, scales = live["aq", h, 2 * c + g]
                nc.tensor.matmul_mx(
                    out=bank[:, qq - lo, :],
                    lhsT=q_words[:, g, 2 * P * qt : 2 * P * (qt + 1)].bitcast(FP4X4),
                    lhsT_scale=q_scales[:, g, P * qt : P * (qt + 1)],
                    rhs=codes[:].bitcast(FP8X4),
                    rhs_scale=scales[:],
                    start=(g == 0),
                    stop=(g == 1),
                )

        def window(h, b, lo, hi):
            c, qh = b // 2, b % 2
            return slice(4 * qh + lo, 4 * qh + hi), slice(256 * h + P * c, 256 * h + P * (c + 1))

        def expo(h, b, lo=0, hi=4):
            e = work.tile([P, hi - lo, P], F32, name="expo", bufs=8)
            live["e", h, b, lo] = e
            nc.scalar.activation(out=e[:], in_=live["z", h, b, lo][:], func=ACT.Exp, scale=1.0 / C)

        def masked(h, b, eng, lo=0, hi=4):
            e = live["e", h, b, lo]
            rows, cols = window(h, b, lo, hi)
            engine = nc.vector if eng == "V" else nc.gpsimd
            engine.tensor_tensor(out=e[:], in0=e[:], in1=mask_sb[:, rows, cols], op=ALU.mult)

        def store(h, b, lo=0, hi=4):
            rows, cols = window(h, b, lo, hi)
            nc.sync.dma_start(out=out_view[:, rows, cols], in_=live["e", h, b, lo][:])

        for task in build_order():
            kind = task[0]
            if kind == "L":
                load(task[1])
            elif kind == "W":
                widen(*task[1:])
            else:
                {"T": turn, "C": copy_out, "Q": quant_x, "M": features, "R": relu_sum, "WI": group_w, "WQ": quant_w,
                 "AQ": quant_a, "Z": scores, "E": expo, "K": masked, "ST": store}[kind](*task[1:])
